import numpy as np
import ml_dtypes


def mxq(x, axis, fmt="e4m3"):
    dtype, down = {"e4m3": (ml_dtypes.float8_e4m3fn, 7), "e5m2": (ml_dtypes.float8_e5m2, 14)}[fmt]
    v = np.moveaxis(np.asarray(x, np.float32).astype(ml_dtypes.bfloat16).astype(np.float64), axis, -1)
    blocks = v.reshape(v.shape[:-1] + (-1, 32))
    amax = np.abs(blocks).max(-1, keepdims=True)
    byte = np.maximum(np.where(amax > 0, np.frexp(amax)[1] - 1 + 127, 0) - down, 1)
    scale = np.exp2(byte - 127.0)
    codes = (blocks / scale).astype(np.float32).astype(dtype).astype(np.float64)
    return np.moveaxis((codes * scale).reshape(v.shape), -1, axis)


WIDE = False


def mx_kscale(k):
    if not WIDE:
        return np.ones(k)
    levels = np.array([30, -30])
    if k % 512:
        return np.exp2(np.random.permutation(np.resize(levels, k // 32))).repeat(32)
    a = np.empty((k // 512, 16))
    for p in range(k // 512):
        a[p, :8] = np.random.permutation(np.resize(levels, 8))
        for g in range(8):
            far = levels[np.abs(levels - a[p, g]) >= 10]
            a[p, g + 8] = far[np.random.randint(len(far))]
    return np.exp2(a.ravel()).repeat(32)


BF16 = ml_dtypes.bfloat16


def bf(x):
    return np.asarray(x, np.float32).astype(BF16)


def f64(x):
    return np.asarray(x).astype(np.float64)


E2M1 = np.array([0.0, 0.5, 1.0, 1.5, 2.0, 3.0, 4.0, 6.0, -0.0, -0.5, -1.0, -1.5, -2.0, -3.0, -4.0, -6.0])


def pack_weight(w, fmt):
    k, n = w.shape
    w = f64(bf(w)).reshape(k // 32, 32, n)
    amax = np.abs(w).max(1)
    if fmt == "e4m3":
        byte = np.frexp(amax)[1] - 1 + 127 - 7
    else:
        mant, ex = np.frexp(amax / 6.0)
        byte = np.where(mant > 0.5, ex, ex - 1) + 127
    byte = np.clip(np.where(amax > 0, byte, 1), 1, 254)
    scaled = (w * np.exp2(127.0 - byte)[:, None, :]).reshape(k, n).astype(np.float32)
    by_word = np.ascontiguousarray(scaled.reshape(k // 512, 128, 4, n).transpose(0, 1, 3, 2))
    if fmt == "e4m3":
        words = by_word.astype(ml_dtypes.float8_e4m3fn).view(np.uint8)
    else:
        c = by_word.astype(ml_dtypes.float4_e2m1fn).view(np.uint8) & 0xF
        words = c[..., 0::2] | (c[..., 1::2] << 4)
    return np.ascontiguousarray(words), np.ascontiguousarray(byte.astype(np.uint8).reshape(k // 512, 16, n))


def unpack_weight(words, scales, fmt):
    g, p, n, _ = words.shape
    if fmt == "e4m3":
        vals = np.ascontiguousarray(words).view(ml_dtypes.float8_e4m3fn).astype(np.float64)
    else:
        nib = np.empty((g, p, n, 4), np.uint8)
        nib[..., 0::2] = words & 0xF
        nib[..., 1::2] = words >> 4
        vals = E2M1[nib]
    vals = vals * np.repeat(np.exp2(scales.astype(np.float64) - 127.0), 8, axis=1)[..., None]
    return vals.transpose(0, 1, 3, 2).reshape(g * 512, n)
def pack4(w):
    words, scales = pack_weight(w, "e2m1")
    return words.reshape(words.shape[0], 128, -1), scales


def unpack4(words, scales):
    return unpack_weight(words.reshape(words.shape[0], 128, -1, 2), scales, "e2m1")


N, K = 1024, 512


def setup_inputs():
    s = mx_kscale(K)
    r = mx_kscale(N)
    v = np.random.standard_normal((K, N)) / np.sqrt(K) / s[:, None]
    v_words, v_scales = pack4(v)
    return {"coef": bf(np.random.standard_normal((N, K)) * s),
            "v_words": v_words,
            "v_scales": v_scales,
            "a": bf(np.random.standard_normal((N, N)) / r[:, None]),
            "b": bf(np.random.standard_normal((N, N)) / r),
            "d": bf(np.random.standard_normal((N, N)) / np.sqrt(N) * r),
            "rjac": bf(1 + 0.1 * np.random.standard_normal((N, N)))}


def reference(coef, v_words, v_scales, a, b, d, rjac):
    u = mxq(f64(coef), 1, "e4m3") @ unpack4(v_words, v_scales)
    fx = f64(a) * u
    fy = f64(b) * u
    dq = mxq(f64(d), 1, "e4m3")
    dx = dq @ mxq(fx, 0, "e5m2")
    dy = mxq(fy, 1, "e5m2") @ dq.T
    return f64(rjac) * (dx + dy)

@@ -1,0 +1,346 @@
+from contextlib import ExitStack
+
+import concourse.mybir as mybir
+from concourse.masks import make_identity
+
+N, K = 1024, 512
+FLOPS = 2 * N * K * N + 2 * 2 * N * N * N
+
+F32 = mybir.dt.float32
+BF16 = mybir.dt.bfloat16
+I32 = mybir.dt.int32
+U32 = mybir.dt.uint32
+U8 = mybir.dt.uint8
+E4 = mybir.dt.float8_e4m3fn_x4
+E5 = mybir.dt.float8_e5m2_x4
+E2 = mybir.dt.float4_e2m1fn_x4
+MULT = mybir.AluOpType.mult
+
+P = 128
+H = 512
+
+
+def tile_spectral_flux_divergence_s9_kernel(tc, coef, v_words, v_scales, a, b, d, rjac, out):
+    nc = tc.nc
+    with ExitStack() as ctx:
+        sb = ctx.enter_context(tc.tile_pool(name="sb", bufs=1))
+        ps = ctx.enter_context(tc.psum_pool(name="ps", bufs=1))
+        ctx.enter_context(tc.manual_schedule())
+
+        def sbt(name, shape, dtype):
+            return sb.tile(shape, dtype, name=name, tag=name, align_bytes=64)
+
+        banks = [ps.tile([P, H], F32, name="bank%d" % i, tag="bank%d" % i) for i in range(8)]
+        two = range(2)
+        four = range(4)
+        quads = [(x, y) for x in two for y in two]
+
+        ident = sbt("ident", [P, P], F32)
+        v_plane = sbt("v_plane", [P, N], U8)
+        v_codes = [sbt("v_codes%d" % h, [P, 2 * H], U8) for h in two]
+        coef_raw = {q: sbt("coef_raw%d%d" % q, [P, 2, K], BF16) for q in quads}
+        coef_bf = {q: sbt("coef_bf%d%d" % q, [P, 4 * 256], BF16) for q in quads}
+        coef_q = {q: sbt("coef_q%d%d" % q, [P, 256], U32) for q in quads}
+        coef_s = {q: sbt("coef_s%d%d" % q, [P, 256], U8) for q in quads}
+        d_raw = [sbt("d_raw%d" % rp, [P, 2, N], BF16) for rp in four]
+        d_sorted = [sbt("d_sorted%d" % rp, [P, 2, N // 2], F32) for rp in four]
+        a_raw = {q: sbt("a_raw%d%d" % q, [P, 4, H], BF16) for q in quads}
+        b_raw = {q: sbt("b_raw%d%d" % q, [P, 4, H], BF16) for q in quads}
+        r_raw = {q: sbt("r_raw%d%d" % q, [P, 4, H], BF16) for q in quads}
+        fy = {(g, h, t): sbt("fy%d%d%d" % (g, h, t), [P, H], BF16) for g, h in quads for t in four}
+        staged, codes, scales = {}, {}, {}
+        for kind in ("dt", "fx", "fyt"):
+            for q in quads:
+                staged[kind, q] = sbt(kind + "_bf%d%d" % q, [P, 4 * H], BF16)
+                codes[kind, q] = sbt(kind + "_q%d%d" % q, [P, H], U32)
+                scales[kind, q] = sbt(kind + "_s%d%d" % q, [P, H], U8)
+        slots = [sbt("res%d" % i, [P, H], F32) for i in range(8)]
+        result = {(r, h): slots[r] for r in range(8) for h in two}
+
+        def half(x):
+            return slice(H * x, H * (x + 1))
+
+        def load_coef(g, tp):
+            src = coef[half(g), :].rearrange("(p t) k -> p t k", t=4)[:, 2 * tp : 2 * tp + 2, :]
+            nc.sync.dma_start(out=coef_raw[g, tp][:], in_=src)
+
+        def load_v(h):
+            nc.sync.dma_start(out=v_codes[h][:].bitcast(I32), in_=v_words[0][:, 2 * H * h : 2 * H * (h + 1)].bitcast(I32))
+
+        def load_factor(tiles, src, g, h):
+            nc.sync.dma_start(out=tiles[g, h][:], in_=src[half(g), half(h)].rearrange("(p t) j -> p t j", t=4))
+
+        def load_d(rp):
+            nc.sync.dma_start(out=d_raw[rp][:], in_=d[256 * rp : 256 * (rp + 1), :].rearrange("(r p) m -> p r m", p=P))
+
+        def load_rjac(g, h):
+            nc.sync.dma_start(out=r_raw[g, h][:], in_=rjac[half(g), half(h)].rearrange("(r p) j -> p r j", p=P))
+
+        nc.vector.memset(v_plane[:].bitcast(U32), 0)
+        make_identity(nc, ident[:])
+        load_coef(0, 0)
+        load_v(0)
+        for q in four:
+            nc.scalar.dma_start(
+                out=v_plane[32 * q : 32 * q + 4, :].bitcast(I32), in_=v_scales[0][4 * q : 4 * q + 4, :].bitcast(I32)
+            )
+        load_coef(0, 1)
+        load_factor(b_raw, b, 0, 0)
+        load_d(0)
+        load_v(1)
+        load_factor(b_raw, b, 0, 1)
+        load_d(1)
+        load_factor(a_raw, a, 0, 0)
+        load_coef(1, 0)
+        load_coef(1, 1)
+        load_d(2)
+        load_factor(a_raw, a, 1, 0)
+        load_d(3)
+        load_factor(b_raw, b, 1, 0)
+        load_rjac(0, 0)
+        load_factor(b_raw, b, 1, 1)
+        load_factor(a_raw, a, 0, 1)
+        load_rjac(1, 0)
+        load_factor(a_raw, a, 1, 1)
+        load_rjac(0, 1)
+        load_rjac(1, 1)
+
+        def turn_input(bank, rows, g, dst, engine_copy):
+            words = rows[:].bitcast(F32)
+            for r in two:
+                for u in two:
+                    x = 2 * r + u
+                    nc.tensor.transpose(bank[:, P * x : P * (x + 1)], words[:, r, 256 * g + u : 256 * (g + 1) : 2], ident[:])
+            engine_copy(
+                out=dst.bitcast(F32).rearrange("p (r c u) -> p r c u", r=2, u=2),
+                in_=bank[:].rearrange("p (r u c) -> p r c u", r=2, u=2),
+            )
+
+        def turn_coef(bank, g, tp, engine_copy):
+            turn_input(bank, coef_raw[g, tp], 0, coef_bf[g, tp][:], engine_copy)
+
+        def sort_d(rp):
+            nc.scalar.copy(
+                out=d_sorted[rp][:].rearrange("p r (g u w) -> p (r g) u w", g=2, u=2),
+                in_=d_raw[rp][:].bitcast(F32).rearrange("p r (g w u) -> p (r g) u w", g=2, u=2),
+            )
+
+        def turn_d(bank, rp, g):
+            for r in two:
+                for u in two:
+                    x = 2 * r + u
+                    y = 2 * g + u
+                    if rp < 2:
+                        words = d_raw[rp][:].bitcast(F32)[:, r, 256 * g + u : 256 * (g + 1) : 2]
+                    else:
+                        words = d_sorted[rp][:, r, P * y : P * (y + 1)]
+                    nc.tensor.transpose(bank[:, P * x : P * (x + 1)], words, ident[:])
+
+        def copy_d(bank, rp, g):
+            dst = staged["dt", (g, rp // 2)][:, 1024 * (rp % 2) : 1024 * (rp % 2 + 1)]
+            nc.scalar.copy(
+                out=dst.bitcast(F32).rearrange("p (r c u) -> p r c u", r=2, u=2),
+                in_=bank[:].rearrange("p (r u c) -> p r c u", r=2, u=2),
+            )
+
+        def turn_fy(bank, g, h, tp):
+            for tl in two:
+                words = fy[g, h, 2 * tp + tl][:].bitcast(F32)
+                for u in two:
+                    x = 2 * tl + u
+                    nc.tensor.transpose(bank[:, P * x : P * (x + 1)], words[:, P * u : P * (u + 1)], ident[:])
+            dst = staged["fyt", (h, g)][:].bitcast(F32).rearrange("p (c x) -> p c x", x=8)[:, :, 4 * tp : 4 * tp + 4]
+            nc.scalar.copy(out=dst, in_=bank[:].rearrange("p (x c) -> p c x", x=4))
+
+        def quant_coef(g, tp):
+            nc.vector.quantize_mx(out=coef_q[g, tp][:].bitcast(E4), scales=coef_s[g, tp][:], in_=coef_bf[g, tp][:])
+
+        def quant(kind, x, y):
+            fmt = E4 if kind == "dt" else E5
+            q = (x, y)
+            nc.vector.quantize_mx(out=codes[kind, q][:].bitcast(fmt), scales=scales[kind, q][:], in_=staged[kind, q][:])
+
+        def field_pass(dst, g, t, j0, width):
+            cols = slice(P * (t % 2), P * (t % 2 + 1))
+            h, lo = divmod(j0, H)
+            nc.tensor.matmul_mx(
+                out=dst,
+                lhsT=coef_q[g, t // 2][:, cols].bitcast(E4),
+                lhsT_scale=coef_s[g, t // 2][:, cols],
+                rhs=v_codes[h][:, 2 * lo : 2 * (lo + width)].bitcast(E2),
+                rhs_scale=v_plane[:, j0 : j0 + width],
+                start=True,
+                stop=True,
+            )
+
+        products = (
+            [("fy", 0, h, t) for h in two for t in four]
+            + [("fx", g, 0, c) for g in two for c in four]
+            + [("fy", 1, h, t) for h in two for t in four]
+            + [("fx", g, 1, c) for g in two for c in four]
+        )
+
+        def field(n):
+            if n >= len(products):
+                return
+            kind, g, h, x = products[n]
+            bank = banks[n % 3]
+            if kind == "fy":
+                field_pass(bank[:], g, x, H * h, H)
+            else:
+                for t in four:
+                    field_pass(bank[:, P * t : P * (t + 1)], g, t, H * h + P * x, P)
+
+        def product(n):
+            kind, g, h, x = products[n]
+            bank = banks[n % 3]
+            if kind == "fy":
+                nc.vector.tensor_tensor(
+                    out=fy[g, h, x][:].rearrange("p (u w e) -> p u w e", u=2, e=2),
+                    in0=bank[:].rearrange("p (w u e) -> p u w e", u=2, e=2),
+                    in1=b_raw[g, h][:, x, :].rearrange("p (w u e) -> p u w e", u=2, e=2),
+                    op=MULT,
+                )
+            else:
+                nc.vector.tensor_tensor(
+                    out=staged["fx", (g, h)][:, H * x : H * (x + 1)].rearrange("p (c i t) -> p c t i", i=4, t=4),
+                    in0=bank[:].rearrange("p (t c i) -> p c t i", t=4, i=4),
+                    in1=a_raw[g, h][:, :, P * x : P * (x + 1)].rearrange("p t (c i) -> p c t i", i=4),
+                    op=MULT,
+                )
+
+        started = set()
+        count = {}
+
+        def flux_pass(bank, r, h, which, s):
+            big, cols = r // 4, slice(P * (r % 4), P * (r % 4 + 1))
+            if which == "x":
+                left, right, lf, rf = ("dt", (s, big)), ("fx", (s, h)), E4, E5
+            else:
+                left, right, lf, rf = ("fyt", (s, big)), ("dt", (s, h)), E5, E4
+            count[r, h] = count.get((r, h), 0) + 1
+            nc.tensor.matmul_mx(
+                out=bank[:],
+                lhsT=codes[left][:, cols].bitcast(lf),
+                lhsT_scale=scales[left][:, cols],
+                rhs=codes[right][:].bitcast(rf),
+                rhs_scale=scales[right][:],
+                start=count[r, h] == 1,
+                stop=count[r, h] == 4,
+            )
+
+        def finish(bank, r, h):
+            nc.vector.tensor_tensor(out=result[r, h][:], in0=bank[:], in1=r_raw[r // 4, h][:, r % 4, :], op=MULT)
+            nc.sync.dma_start(out=out[P * r : P * (r + 1), half(h)], in_=result[r, h][:])
+
+        def step(n):
+            product(n)
+
+        acc = banks[4:8]
+        tb = banks[3]
+
+        def td(bank, rp, g):
+            turn_d(bank, rp, g)
+            copy_d(bank, rp, g)
+
+        def passes(bank, r, h, *names):
+            for w in names:
+                flux_pass(bank, r, h, w[0], int(w[1]))
+
+        turn_coef(banks[3], 0, 0, nc.scalar.copy)
+        turn_coef(banks[4], 0, 1, nc.scalar.copy)
+        quant_coef(0, 0)
+        field(0)
+        field(1)
+        quant_coef(0, 1)
+        field(2)
+        product(0); field(3)
+        product(1); field(4); td(banks[5], 0, 0); td(banks[6], 0, 1)
+        product(2); field(5)
+        product(3); field(6); td(banks[7], 1, 0); td(banks[3], 1, 1)
+        product(4); field(7); turn_fy(banks[4], 0, 0, 0); turn_fy(banks[5], 0, 0, 1)
+        product(5); field(8)
+        product(6); field(9); turn_coef(banks[6], 1, 0, nc.scalar.copy); turn_coef(banks[7], 1, 1, nc.scalar.copy)
+        quant("dt", 0, 0)
+        product(7); field(10)
+        quant("dt", 1, 0)
+        product(8); field(11); turn_fy(banks[3], 0, 1, 0); turn_fy(banks[4], 0, 1, 1)
+        quant("fyt", 0, 0)
+        sort_d(2)
+        sort_d(3)
+        product(9)
+        quant_coef(1, 0)
+        quant_coef(1, 1)
+        field(12)
+        passes(acc[1], 1, 0, "y0"); passes(acc[2], 2, 0, "y0"); passes(acc[3], 3, 0, "y0")
+        product(10); field(13)
+        product(11); field(14)
+        quant("fyt", 1, 0)
+        passes(acc[1], 1, 0, "y1"); passes(acc[2], 2, 0, "y1"); passes(acc[3], 3, 0, "y1")
+        product(12); field(15); td(banks[3], 2, 0); td(banks[4], 3, 0)
+        quant("fx", 0, 0)
+        passes(acc[1], 1, 0, "x0"); passes(acc[2], 2, 0, "x0"); passes(acc[3], 3, 0, "x0")
+        product(13); field(16); td(banks[3], 2, 1); td(banks[4], 3, 1)
+        product(14); field(17)
+        product(15); field(18)
+        passes(acc[0], 0, 0, "y0", "y1", "x0")
+        product(16); field(19)
+        quant("fx", 1, 0)
+        for r in (1, 2, 3, 0):
+            passes(acc[r], r, 0, "x1")
+        product(17); field(20); turn_fy(tb, 1, 0, 0)
+        quant("dt", 0, 1)
+        finish(acc[1], 1, 0)
+        quant("dt", 1, 1)
+        product(18); field(21)
+        passes(acc[1], 5, 0, "x0", "x1")
+        finish(acc[2], 2, 0)
+        product(19); field(22); turn_fy(tb, 1, 0, 1)
+        passes(acc[2], 6, 0, "x0", "x1")
+        finish(acc[3], 3, 0)
+        product(20); field(23)
+        passes(acc[3], 7, 0, "x0", "x1")
+        finish(acc[0], 0, 0)
+        product(21); field(24); turn_fy(tb, 1, 1, 0)
+        passes(acc[0], 4, 0, "x0", "x1")
+        product(22); field(25)
+        quant("fyt", 0, 1)
+        passes(acc[1], 5, 0, "y0"); passes(acc[2], 6, 0, "y0")
+        product(23); field(26); turn_fy(tb, 1, 1, 1)
+        passes(acc[3], 7, 0, "y0"); passes(acc[0], 4, 0, "y0")
+        product(24); field(27)
+        product(25); field(28)
+        last = [tb, acc[1], acc[2], acc[3], acc[0]] + [banks[2], banks[0], banks[1]]
+        passes(last[0], 0, 1, "y0", "y1")
+        product(26); field(29)
+        quant("fyt", 1, 1)
+        for r in (1, 2, 3, 0):
+            passes(acc[r], 4 + r, 0, "y1")
+        product(27); field(30)
+        finish(acc[1], 5, 0)
+        quant("fx", 0, 1)
+        passes(last[1], 1, 1, "y0", "y1")
+        finish(acc[2], 6, 0)
+        product(28); field(31)
+        passes(last[2], 2, 1, "y0", "y1")
+        finish(acc[3], 7, 0)
+        product(29)
+        passes(last[0], 0, 1, "x0"); passes(last[1], 1, 1, "x0"); passes(last[2], 2, 1, "x0")
+        finish(acc[0], 4, 0)
+        passes(last[3], 3, 1, "y0", "y1", "x0")
+        product(30)
+        passes(last[4], 4, 1, "y0", "y1", "x0")
+        product(31)
+        quant("fx", 1, 1)
+        passes(last[5], 5, 1, "y0", "y1", "x0")
+        for r in range(3):
+            passes(last[r], r, 1, "x1")
+            finish(last[r], r, 1)
+        passes(last[6], 6, 1, "y0", "y1")
+        for r in range(3, 6):
+            passes(last[r], r, 1, "x1")
+            finish(last[r], r, 1)
+        passes(last[6], 6, 1, "x0", "x1")
+        finish(last[6], 6, 1)
+        passes(last[7], 7, 1, "y0", "y1", "x0", "x1")
+        finish(last[7], 7, 1)

@@ -43,7 +43,8 @@ def tile_spectral_flux_divergence_s9_kernel(tc, coef, v_words, v_scales, a, b, d
         coef_q = {q: sbt("coef_q%d%d" % q, [P, 256], U32) for q in quads}
         coef_s = {q: sbt("coef_s%d%d" % q, [P, 256], U8) for q in quads}
         d_raw = [sbt("d_raw%d" % rp, [P, 2, N], BF16) for rp in four]
-        d_sorted = [sbt("d_sorted%d" % rp, [P, 2, N // 2], F32) for rp in four]
+        d_pair = [sbt("d_sorted%d" % rp, [P, 2, N // 2], F32) for rp in two]
+        d_sorted = d_pair + d_pair
         a_raw = {q: sbt("a_raw%d%d" % q, [P, 4, H], BF16) for q in quads}
         b_raw = {q: sbt("b_raw%d%d" % q, [P, 4, H], BF16) for q in quads}
         r_raw = {q: sbt("r_raw%d%d" % q, [P, 4, H], BF16) for q in quads}
@@ -80,21 +81,21 @@ def tile_spectral_flux_divergence_s9_kernel(tc, coef, v_words, v_scales, a, b, d
         make_identity(nc, ident[:])
         load_coef(0, 0)
         load_v(0)
+        load_coef(0, 1)
         for q in four:
-            nc.scalar.dma_start(
+            nc.sync.dma_start(
                 out=v_plane[32 * q : 32 * q + 4, :].bitcast(I32), in_=v_scales[0][4 * q : 4 * q + 4, :].bitcast(I32)
             )
-        load_coef(0, 1)
         load_factor(b_raw, b, 0, 0)
         load_d(0)
         load_v(1)
         load_factor(b_raw, b, 0, 1)
-        load_d(1)
-        load_factor(a_raw, a, 0, 0)
         load_coef(1, 0)
         load_coef(1, 1)
-        load_d(2)
+        load_factor(a_raw, a, 0, 0)
+        load_d(1)
         load_factor(a_raw, a, 1, 0)
+        load_d(2)
         load_d(3)
         load_factor(b_raw, b, 1, 0)
         load_rjac(0, 0)
@@ -130,11 +131,7 @@ def tile_spectral_flux_divergence_s9_kernel(tc, coef, v_words, v_scales, a, b, d
                 for u in two:
                     x = 2 * r + u
                     y = 2 * g + u
-                    if rp < 2:
-                        words = d_raw[rp][:].bitcast(F32)[:, r, 256 * g + u : 256 * (g + 1) : 2]
-                    else:
-                        words = d_sorted[rp][:, r, P * y : P * (y + 1)]
-                    nc.tensor.transpose(bank[:, P * x : P * (x + 1)], words, ident[:])
+                    nc.tensor.transpose(bank[:, P * x : P * (x + 1)], d_sorted[rp][:, r, P * y : P * (y + 1)], ident[:])
 
         def copy_d(bank, rp, g):
             dst = staged["dt", (g, rp // 2)][:, 1024 * (rp % 2) : 1024 * (rp % 2 + 1)]
@@ -142,6 +139,11 @@ def tile_spectral_flux_divergence_s9_kernel(tc, coef, v_words, v_scales, a, b, d
                 out=dst.bitcast(F32).rearrange("p (r c u) -> p r c u", r=2, u=2),
                 in_=bank[:].rearrange("p (r u c) -> p r c u", r=2, u=2),
             )
+
+        def td(bank, rp, g):
+            turn_d(bank, rp, g)
+            copy_d(bank, rp, g)
+
 
         def turn_fy(bank, g, h, tp):
             for tl in two:
@@ -180,11 +182,15 @@ def tile_spectral_flux_divergence_s9_kernel(tc, coef, v_words, v_scales, a, b, d
             + [("fx", g, 1, c) for g in two for c in four]
         )
 
+        idle = list(banks)
+        held = {}
+
         def field(n):
             if n >= len(products):
                 return
             kind, g, h, x = products[n]
-            bank = banks[n % 3]
+            bank = idle.pop(0)
+            held[n] = bank
             if kind == "fy":
                 field_pass(bank[:], g, x, H * h, H)
             else:
@@ -193,7 +199,7 @@ def tile_spectral_flux_divergence_s9_kernel(tc, coef, v_words, v_scales, a, b, d
 
         def product(n):
             kind, g, h, x = products[n]
-            bank = banks[n % 3]
+            bank = held[n]
             if kind == "fy":
                 nc.vector.tensor_tensor(
                     out=fy[g, h, x][:].rearrange("p (u w e) -> p u w e", u=2, e=2),
@@ -239,108 +245,149 @@ def tile_spectral_flux_divergence_s9_kernel(tc, coef, v_words, v_scales, a, b, d
         acc = banks[4:8]
         tb = banks[3]
 
-        def td(bank, rp, g):
-            turn_d(bank, rp, g)
-            copy_d(bank, rp, g)
-
-        def passes(bank, r, h, *names):
+        def passes(r, h, *names):
+            if (r, h) not in held:
+                held[r, h] = idle.pop(0)
             for w in names:
-                flux_pass(bank, r, h, w[0], int(w[1]))
+                flux_pass(held[r, h], r, h, w[0], int(w[1]))
 
-        turn_coef(banks[3], 0, 0, nc.scalar.copy)
-        turn_coef(banks[4], 0, 1, nc.scalar.copy)
+        def prod(n):
+            product(n)
+            idle.append(held[n])
+
+        def fin(r, h):
+            finish(held[r, h], r, h)
+            idle.append(held[r, h])
+
+        def turns(*jobs):
+            for job in jobs:
+                bank = idle.pop(0)
+                if job[0] == "c":
+                    turn_coef(bank, job[1], job[2], nc.scalar.copy)
+                elif job[0] == "d":
+                    td(bank, job[1], job[2])
+                else:
+                    turn_fy(bank, job[1], job[2], job[3])
+                idle.append(bank)
+
+        turns(("c", 0, 0), ("c", 0, 1))
         quant_coef(0, 0)
-        field(0)
-        field(1)
+        field(0); field(1)
         quant_coef(0, 1)
-        field(2)
-        product(0); field(3)
-        product(1); field(4); td(banks[5], 0, 0); td(banks[6], 0, 1)
-        product(2); field(5)
-        product(3); field(6); td(banks[7], 1, 0); td(banks[3], 1, 1)
-        product(4); field(7); turn_fy(banks[4], 0, 0, 0); turn_fy(banks[5], 0, 0, 1)
-        product(5); field(8)
-        product(6); field(9); turn_coef(banks[6], 1, 0, nc.scalar.copy); turn_coef(banks[7], 1, 1, nc.scalar.copy)
-        quant("dt", 0, 0)
-        product(7); field(10)
-        quant("dt", 1, 0)
-        product(8); field(11); turn_fy(banks[3], 0, 1, 0); turn_fy(banks[4], 0, 1, 1)
+        field(2); field(3); field(4); field(5)
+        sort_d(0)
+        prod(0)
+        prod(1)
+        turns(("d", 0, 0), ("d", 0, 1))
+        field(6); field(7)
+        prod(2)
+        prod(3)
+        turns(("y", 0, 0, 0), ("y", 0, 0, 1))
+        sort_d(1)
+        prod(4)
+        field(8); field(9)
+        prod(5)
+        turns(("c", 1, 0), ("c", 1, 1))
+        prod(6)
+        prod(7)
+        field(10); field(11)
+        turns(("d", 1, 0), ("d", 1, 1))
+        prod(8)
         quant("fyt", 0, 0)
-        sort_d(2)
-        sort_d(3)
-        product(9)
+        prod(9)
+        prod(10)
         quant_coef(1, 0)
         quant_coef(1, 1)
         field(12)
-        passes(acc[1], 1, 0, "y0"); passes(acc[2], 2, 0, "y0"); passes(acc[3], 3, 0, "y0")
-        product(10); field(13)
-        product(11); field(14)
-        quant("fyt", 1, 0)
-        passes(acc[1], 1, 0, "y1"); passes(acc[2], 2, 0, "y1"); passes(acc[3], 3, 0, "y1")
-        product(12); field(15); td(banks[3], 2, 0); td(banks[4], 3, 0)
+        turns(("y", 0, 1, 0), ("y", 0, 1, 1))
+        sort_d(2)
+        sort_d(3)
+        field(13)
+        prod(11)
+        quant("dt", 0, 0)
+        field(14)
+        passes(0, 0, "y0"); passes(1, 0, "y0"); passes(2, 0, "y0")
+        prod(12)
         quant("fx", 0, 0)
-        passes(acc[1], 1, 0, "x0"); passes(acc[2], 2, 0, "x0"); passes(acc[3], 3, 0, "x0")
-        product(13); field(16); td(banks[3], 2, 1); td(banks[4], 3, 1)
-        product(14); field(17)
-        product(15); field(18)
-        passes(acc[0], 0, 0, "y0", "y1", "x0")
-        product(16); field(19)
+        field(15)
+        passes(0, 0, "x0"); passes(1, 0, "x0"); passes(2, 0, "x0")
+        quant("dt", 1, 0)
+        prod(13)
+        quant("fyt", 1, 0)
+        field(16)
+        turns(("d", 2, 0), ("d", 2, 1))
+        passes(0, 0, "y1"); passes(1, 0, "y1"); passes(2, 0, "y1")
+        prod(14)
+        field(17)
+        prod(15)
+        field(18)
+        turns(("d", 3, 0), ("d", 3, 1))
+        prod(16)
         quant("fx", 1, 0)
-        for r in (1, 2, 3, 0):
-            passes(acc[r], r, 0, "x1")
-        product(17); field(20); turn_fy(tb, 1, 0, 0)
+        passes(0, 0, "x1"); passes(1, 0, "x1"); passes(2, 0, "x1")
+        prod(17)
+        field(19)
+        passes(3, 0, "y0", "x0", "y1", "x1")
+        prod(18)
+        fin(0, 0)
+        field(20)
         quant("dt", 0, 1)
-        finish(acc[1], 1, 0)
+        fin(1, 0)
+        field(21)
+        prod(19)
         quant("dt", 1, 1)
-        product(18); field(21)
-        passes(acc[1], 5, 0, "x0", "x1")
-        finish(acc[2], 2, 0)
-        product(19); field(22); turn_fy(tb, 1, 0, 1)
-        passes(acc[2], 6, 0, "x0", "x1")
-        finish(acc[3], 3, 0)
-        product(20); field(23)
-        passes(acc[3], 7, 0, "x0", "x1")
-        finish(acc[0], 0, 0)
-        product(21); field(24); turn_fy(tb, 1, 1, 0)
-        passes(acc[0], 4, 0, "x0", "x1")
-        product(22); field(25)
+        turns(("y", 1, 0, 0), ("y", 1, 0, 1))
+        passes(4, 0, "x0", "x1")
+        fin(2, 0)
+        field(22)
+        passes(5, 0, "x0", "x1")
+        prod(20)
+        fin(3, 0)
+        field(23)
+        passes(6, 0, "x0", "x1")
+        prod(21)
         quant("fyt", 0, 1)
-        passes(acc[1], 5, 0, "y0"); passes(acc[2], 6, 0, "y0")
-        product(23); field(26); turn_fy(tb, 1, 1, 1)
-        passes(acc[3], 7, 0, "y0"); passes(acc[0], 4, 0, "y0")
-        product(24); field(27)
-        product(25); field(28)
-        last = [tb, acc[1], acc[2], acc[3], acc[0]] + [banks[2], banks[0], banks[1]]
-        passes(last[0], 0, 1, "y0", "y1")
-        product(26); field(29)
+        field(24)
+        turns(("y", 1, 1, 0))
+        passes(7, 0, "x0", "x1")
+        prod(22)
+        field(25)
+        passes(4, 0, "y0"); passes(5, 0, "y0")
+        prod(23)
+        field(26)
+        turns(("y", 1, 1, 1))
+        passes(6, 0, "y0"); passes(7, 0, "y0")
+        prod(24)
+        field(27)
+        prod(25)
+        passes(0, 1, "y0", "y1")
+        field(28)
+        prod(26)
         quant("fyt", 1, 1)
-        for r in (1, 2, 3, 0):
-            passes(acc[r], 4 + r, 0, "y1")
-        product(27); field(30)
-        finish(acc[1], 5, 0)
+        for r in range(4, 8):
+            passes(r, 0, "y1")
+        prod(27)
+        field(29)
+        fin(4, 0)
         quant("fx", 0, 1)
-        passes(last[1], 1, 1, "y0", "y1")
-        finish(acc[2], 6, 0)
-        product(28); field(31)
-        passes(last[2], 2, 1, "y0", "y1")
-        finish(acc[3], 7, 0)
-        product(29)
-        passes(last[0], 0, 1, "x0"); passes(last[1], 1, 1, "x0"); passes(last[2], 2, 1, "x0")
-        finish(acc[0], 4, 0)
-        passes(last[3], 3, 1, "y0", "y1", "x0")
-        product(30)
-        passes(last[4], 4, 1, "y0", "y1", "x0")
-        product(31)
+        field(30)
+        passes(1, 1, "y0", "y1")
+        fin(5, 0)
+        passes(2, 1, "y0", "y1")
+        prod(28)
+        field(31)
+        fin(6, 0)
+        passes(3, 1, "y0", "y1")
+        prod(29)
+        passes(0, 1, "x0"); passes(1, 1, "x0"); passes(2, 1, "x0"); passes(3, 1, "x0")
+        prod(30)
+        passes(4, 1, "y0", "y1", "x0")
+        prod(31)
+        passes(5, 1, "y0", "y1")
+        fin(7, 0)
         quant("fx", 1, 1)
-        passes(last[5], 5, 1, "y0", "y1", "x0")
-        for r in range(3):
-            passes(last[r], r, 1, "x1")
-            finish(last[r], r, 1)
-        passes(last[6], 6, 1, "y0", "y1")
-        for r in range(3, 6):
-            passes(last[r], r, 1, "x1")
-            finish(last[r], r, 1)
-        passes(last[6], 6, 1, "x0", "x1")
-        finish(last[6], 6, 1)
-        passes(last[7], 7, 1, "y0", "y1", "x0", "x1")
-        finish(last[7], 7, 1)
+        passes(0, 1, "x1"); passes(1, 1, "x1"); passes(5, 1, "x0"); passes(2, 1, "x1")
+        passes(6, 1, "y0"); passes(3, 1, "x1"); passes(6, 1, "y1"); passes(4, 1, "x1"); passes(6, 1, "x0"); passes(5, 1, "x1")
+        passes(6, 1, "x1"); passes(7, 1, "y0", "y1", "x0", "x1")
+        for r in range(8):
+            fin(r, 1)

@@ -43,6 +43,7 @@ def tile_spectral_flux_divergence_s9_kernel(tc, coef, v_words, v_scales, a, b, d
         coef_q = {q: sbt("coef_q%d%d" % q, [P, 256], U32) for q in quads}
         coef_s = {q: sbt("coef_s%d%d" % q, [P, 256], U8) for q in quads}
         d_raw = [sbt("d_raw%d" % rp, [P, 2, N], BF16) for rp in four]
+        kept = {(1, 0): sbt("kept10", [P, 4, H], F32)}
         d_pair = [sbt("d_sorted%d" % rp, [P, 2, N // 2], F32) for rp in two]
         d_sorted = d_pair + d_pair
         a_raw = {q: sbt("a_raw%d%d" % q, [P, 4, H], BF16) for q in quads}
@@ -90,16 +91,16 @@ def tile_spectral_flux_divergence_s9_kernel(tc, coef, v_words, v_scales, a, b, d
         load_d(0)
         load_v(1)
         load_factor(b_raw, b, 0, 1)
+        load_d(1)
+        load_factor(a_raw, a, 0, 0)
         load_coef(1, 0)
         load_coef(1, 1)
-        load_factor(a_raw, a, 0, 0)
-        load_d(1)
-        load_factor(a_raw, a, 1, 0)
         load_d(2)
         load_d(3)
+        load_factor(a_raw, a, 1, 0)
+        load_factor(b_raw, b, 1, 1)
         load_factor(b_raw, b, 1, 0)
         load_rjac(0, 0)
-        load_factor(b_raw, b, 1, 1)
         load_factor(a_raw, a, 0, 1)
         load_rjac(1, 0)
         load_factor(a_raw, a, 1, 1)
@@ -131,7 +132,11 @@ def tile_spectral_flux_divergence_s9_kernel(tc, coef, v_words, v_scales, a, b, d
                 for u in two:
                     x = 2 * r + u
                     y = 2 * g + u
-                    nc.tensor.transpose(bank[:, P * x : P * (x + 1)], d_sorted[rp][:, r, P * y : P * (y + 1)], ident[:])
+                    if rp == 2:
+                        words = d_raw[rp][:].bitcast(F32)[:, r, 256 * g + u : 256 * (g + 1) : 2]
+                    else:
+                        words = d_sorted[rp][:, r, P * y : P * (y + 1)]
+                    nc.tensor.transpose(bank[:, P * x : P * (x + 1)], words, ident[:])
 
         def copy_d(bank, rp, g):
             dst = staged["dt", (g, rp // 2)][:, 1024 * (rp % 2) : 1024 * (rp % 2 + 1)]
@@ -144,6 +149,20 @@ def tile_spectral_flux_divergence_s9_kernel(tc, coef, v_words, v_scales, a, b, d
             turn_d(bank, rp, g)
             copy_d(bank, rp, g)
 
+        def keep(n):
+            kind, g, h, x = products[n]
+            nc.scalar.copy(
+                out=kept[g, h][:].rearrange("p t (u c w e) -> p t u c w e", u=2, c=4, e=2)[:, :, :, x, :, :],
+                in_=held[n][:].rearrange("p (t w u e) -> p t u w e", t=4, u=2, e=2),
+            )
+
+        def late_fy(engine, g, h, t):
+            engine.tensor_tensor(
+                out=fy[g, h, t][:].rearrange("p (u w e) -> p u w e", u=2, e=2),
+                in0=kept[g, h][:, t, :].rearrange("p (u w e) -> p u w e", u=2, e=2),
+                in1=b_raw[g, h][:, t, :].rearrange("p (w u e) -> p u w e", u=2, e=2),
+                op=MULT,
+            )
 
         def turn_fy(bank, g, h, tp):
             for tl in two:
@@ -178,7 +197,7 @@ def tile_spectral_flux_divergence_s9_kernel(tc, coef, v_words, v_scales, a, b, d
         products = (
             [("fy", 0, h, t) for h in two for t in four]
             + [("fx", g, 0, c) for g in two for c in four]
-            + [("fy", 1, h, t) for h in two for t in four]
+            + [("fy", 1, 1, t) for t in four]
             + [("fx", g, 1, c) for g in two for c in four]
         )
 
@@ -209,9 +228,9 @@ def tile_spectral_flux_divergence_s9_kernel(tc, coef, v_words, v_scales, a, b, d
                 )
             else:
                 nc.vector.tensor_tensor(
-                    out=staged["fx", (g, h)][:, H * x : H * (x + 1)].rearrange("p (c i t) -> p c t i", i=4, t=4),
-                    in0=bank[:].rearrange("p (t c i) -> p c t i", t=4, i=4),
-                    in1=a_raw[g, h][:, :, P * x : P * (x + 1)].rearrange("p t (c i) -> p c t i", i=4),
+                    out=staged["fx", (g, h)][:, H * x : H * (x + 1)].rearrange("p (c i t) -> p c t i", i=2, t=4),
+                    in0=bank[:].rearrange("p (t c i) -> p c t i", t=4, i=2),
+                    in1=a_raw[g, h][:, :, P * x : P * (x + 1)].rearrange("p t (c i) -> p c t i", i=2),
                     op=MULT,
                 )
 
@@ -253,6 +272,8 @@ def tile_spectral_flux_divergence_s9_kernel(tc, coef, v_words, v_scales, a, b, d
 
         def prod(n):
             product(n)
+            if products[n][:3] == ("fx", 1, 0):
+                keep(n)
             idle.append(held[n])
 
         def fin(r, h):
@@ -279,115 +300,104 @@ def tile_spectral_flux_divergence_s9_kernel(tc, coef, v_words, v_scales, a, b, d
         prod(0)
         prod(1)
         turns(("d", 0, 0), ("d", 0, 1))
+        sort_d(1)
         field(6); field(7)
         prod(2)
         prod(3)
-        turns(("y", 0, 0, 0), ("y", 0, 0, 1))
-        sort_d(1)
         prod(4)
-        field(8); field(9)
         prod(5)
-        turns(("c", 1, 0), ("c", 1, 1))
+        field(8)
+        turns(("y", 0, 0, 0), ("y", 0, 0, 1))
+        field(9); field(10)
         prod(6)
         prod(7)
-        field(10); field(11)
         turns(("d", 1, 0), ("d", 1, 1))
+        field(11)
+        turns(("c", 1, 0), ("c", 1, 1))
         prod(8)
-        quant("fyt", 0, 0)
         prod(9)
-        prod(10)
-        quant_coef(1, 0)
-        quant_coef(1, 1)
-        field(12)
-        turns(("y", 0, 1, 0), ("y", 0, 1, 1))
-        sort_d(2)
-        sort_d(3)
-        field(13)
-        prod(11)
-        quant("dt", 0, 0)
-        field(14)
-        passes(0, 0, "y0"); passes(1, 0, "y0"); passes(2, 0, "y0")
-        prod(12)
-        quant("fx", 0, 0)
-        field(15)
-        passes(0, 0, "x0"); passes(1, 0, "x0"); passes(2, 0, "x0")
-        quant("dt", 1, 0)
-        prod(13)
-        quant("fyt", 1, 0)
-        field(16)
         turns(("d", 2, 0), ("d", 2, 1))
-        passes(0, 0, "y1"); passes(1, 0, "y1"); passes(2, 0, "y1")
+        sort_d(3)
+        quant("fyt", 0, 0)
+        prod(10)
+        prod(11)
+        quant_coef(1, 0)
+        field(16)
+        quant("dt", 0, 0)
+        quant_coef(1, 1)
+        field(12); field(13)
+        turns(("y", 0, 1, 0), ("y", 0, 1, 1))
+        quant("fx", 0, 0)
+        field(14); field(15)
+        quant("dt", 1, 0)
+        passes(0, 0, "y0", "x0")
+        prod(12)
+        prod(13)
+        turns(("d", 3, 0), ("d", 3, 1))
+        quant("fyt", 1, 0)
+        passes(1, 0, "y0", "x0"); passes(2, 0, "y0", "x0")
         prod(14)
         field(17)
+        passes(0, 0, "y1"); passes(1, 0, "y1"); passes(2, 0, "y1")
         prod(15)
         field(18)
-        turns(("d", 3, 0), ("d", 3, 1))
-        prod(16)
+        for t in four:
+            late_fy(nc.gpsimd, 1, 0, t)
+        quant("dt", 0, 1)
         quant("fx", 1, 0)
         passes(0, 0, "x1"); passes(1, 0, "x1"); passes(2, 0, "x1")
-        prod(17)
-        field(19)
-        passes(3, 0, "y0", "x0", "y1", "x1")
-        prod(18)
-        fin(0, 0)
-        field(20)
-        quant("dt", 0, 1)
-        fin(1, 0)
-        field(21)
-        prod(19)
         quant("dt", 1, 1)
-        turns(("y", 1, 0, 0), ("y", 1, 0, 1))
+        passes(3, 0, "y0", "x0", "y1", "x1")
+        prod(16)
+        field(19)
+        prod(17)
         passes(4, 0, "x0", "x1")
-        fin(2, 0)
-        field(22)
+        fin(0, 0)
+        prod(18)
+        field(20)
         passes(5, 0, "x0", "x1")
-        prod(20)
-        fin(3, 0)
-        field(23)
+        fin(1, 0)
+        prod(19)
+        field(21)
+        fin(2, 0)
+        turns(("y", 1, 1, 0), ("y", 1, 1, 1))
         passes(6, 0, "x0", "x1")
-        prod(21)
-        quant("fyt", 0, 1)
-        field(24)
-        turns(("y", 1, 1, 0))
+        fin(3, 0)
+        field(22)
         passes(7, 0, "x0", "x1")
-        prod(22)
-        field(25)
-        passes(4, 0, "y0"); passes(5, 0, "y0")
-        prod(23)
-        field(26)
-        turns(("y", 1, 1, 1))
-        passes(6, 0, "y0"); passes(7, 0, "y0")
-        prod(24)
-        field(27)
-        prod(25)
-        passes(0, 1, "y0", "y1")
-        field(28)
-        prod(26)
+        prod(20)
+        prod(21)
+        turns(("y", 1, 0, 0), ("y", 1, 0, 1))
         quant("fyt", 1, 1)
-        for r in range(4, 8):
-            passes(r, 0, "y1")
-        prod(27)
-        field(29)
-        fin(4, 0)
+        field(23)
+        passes(4, 0, "y1"); passes(5, 0, "y1"); passes(6, 0, "y1"); passes(7, 0, "y1")
+        prod(22)
+        field(24)
+        passes(0, 1, "y0", "y1")
+        prod(23)
+        quant("fyt", 0, 1)
+        field(25)
+        passes(4, 0, "y0"); passes(5, 0, "y0"); passes(6, 0, "y0"); passes(7, 0, "y0")
+        field(26)
+        prod(24)
         quant("fx", 0, 1)
-        field(30)
+        fin(4, 0)
+        field(27)
         passes(1, 1, "y0", "y1")
         fin(5, 0)
         passes(2, 1, "y0", "y1")
-        prod(28)
-        field(31)
-        fin(6, 0)
+        prod(25)
         passes(3, 1, "y0", "y1")
-        prod(29)
+        fin(6, 0)
+        prod(26)
         passes(0, 1, "x0"); passes(1, 1, "x0"); passes(2, 1, "x0"); passes(3, 1, "x0")
-        prod(30)
+        prod(27)
         passes(4, 1, "y0", "y1", "x0")
-        prod(31)
-        passes(5, 1, "y0", "y1")
         fin(7, 0)
         quant("fx", 1, 1)
-        passes(0, 1, "x1"); passes(1, 1, "x1"); passes(5, 1, "x0"); passes(2, 1, "x1")
-        passes(6, 1, "y0"); passes(3, 1, "x1"); passes(6, 1, "y1"); passes(4, 1, "x1"); passes(6, 1, "x0"); passes(5, 1, "x1")
-        passes(6, 1, "x1"); passes(7, 1, "y0", "y1", "x0", "x1")
+        for r in range(5):
+            passes(r, 1, "x1")
+        for r in range(5, 8):
+            passes(r, 1, "y0", "y1", "x0", "x1")
         for r in range(8):
             fin(r, 1)

@@ -43,7 +43,7 @@ def tile_spectral_flux_divergence_s9_kernel(tc, coef, v_words, v_scales, a, b, d
         coef_q = {q: sbt("coef_q%d%d" % q, [P, 256], U32) for q in quads}
         coef_s = {q: sbt("coef_s%d%d" % q, [P, 256], U8) for q in quads}
         d_raw = [sbt("d_raw%d" % rp, [P, 2, N], BF16) for rp in four]
-        kept = {(1, 0): sbt("kept10", [P, 4, H], F32)}
+        kept = {(1, h): sbt("kept1%d" % h, [P, 4, H], F32) for h in two}
         d_pair = [sbt("d_sorted%d" % rp, [P, 2, N // 2], F32) for rp in two]
         d_sorted = d_pair + d_pair
         a_raw = {q: sbt("a_raw%d%d" % q, [P, 4, H], BF16) for q in quads}
@@ -57,7 +57,7 @@ def tile_spectral_flux_divergence_s9_kernel(tc, coef, v_words, v_scales, a, b, d
                 codes[kind, q] = sbt(kind + "_q%d%d" % q, [P, H], U32)
                 scales[kind, q] = sbt(kind + "_s%d%d" % q, [P, H], U8)
         slots = [sbt("res%d" % i, [P, H], F32) for i in range(8)]
-        result = {(r, h): slots[r] for r in range(8) for h in two}
+        result = {(r, h): slots[(r % 4) + 4 * h] for r in range(8) for h in two}
 
         def half(x):
             return slice(H * x, H * (x + 1))
@@ -96,15 +96,15 @@ def tile_spectral_flux_divergence_s9_kernel(tc, coef, v_words, v_scales, a, b, d
         load_coef(1, 0)
         load_coef(1, 1)
         load_d(2)
-        load_d(3)
         load_factor(a_raw, a, 1, 0)
-        load_factor(b_raw, b, 1, 1)
+        load_d(3)
+        load_factor(a_raw, a, 1, 1)
         load_factor(b_raw, b, 1, 0)
         load_rjac(0, 0)
         load_factor(a_raw, a, 0, 1)
-        load_rjac(1, 0)
-        load_factor(a_raw, a, 1, 1)
+        load_factor(b_raw, b, 1, 1)
         load_rjac(0, 1)
+        load_rjac(1, 0)
         load_rjac(1, 1)
 
         def turn_input(bank, rows, g, dst, engine_copy):
@@ -196,9 +196,7 @@ def tile_spectral_flux_divergence_s9_kernel(tc, coef, v_words, v_scales, a, b, d
 
         products = (
             [("fy", 0, h, t) for h in two for t in four]
-            + [("fx", g, 0, c) for g in two for c in four]
-            + [("fy", 1, 1, t) for t in four]
-            + [("fx", g, 1, c) for g in two for c in four]
+            + [("fx", g, h, c) for g, h in ((0, 0), (1, 0), (1, 1), (0, 1)) for c in four]
         )
 
         idle = list(banks)
@@ -255,8 +253,14 @@ def tile_spectral_flux_divergence_s9_kernel(tc, coef, v_words, v_scales, a, b, d
             )
 
         def finish(bank, r, h):
-            nc.vector.tensor_tensor(out=result[r, h][:], in0=bank[:], in1=r_raw[r // 4, h][:, r % 4, :], op=MULT)
-            nc.sync.dma_start(out=out[P * r : P * (r + 1), half(h)], in_=result[r, h][:])
+            pieces = 2 if (r, h) == (7, 1) else 1
+            width = H // pieces
+            for s in range(pieces):
+                cols = slice(width * s, width * (s + 1))
+                nc.vector.tensor_tensor(
+                    out=result[r, h][:, cols], in0=bank[:, cols], in1=r_raw[r // 4, h][:, r % 4, cols], op=MULT
+                )
+                nc.sync.dma_start(out=out[P * r : P * (r + 1), half(h)][:, cols], in_=result[r, h][:, cols])
 
         def step(n):
             product(n)
@@ -272,7 +276,7 @@ def tile_spectral_flux_divergence_s9_kernel(tc, coef, v_words, v_scales, a, b, d
 
         def prod(n):
             product(n)
-            if products[n][:3] == ("fx", 1, 0):
+            if products[n][0] == "fx" and products[n][1] == 1:
                 keep(n)
             idle.append(held[n])
 
@@ -295,109 +299,96 @@ def tile_spectral_flux_divergence_s9_kernel(tc, coef, v_words, v_scales, a, b, d
         quant_coef(0, 0)
         field(0); field(1)
         quant_coef(0, 1)
-        field(2); field(3); field(4); field(5)
+        for n in range(2, 8):
+            field(n)
         sort_d(0)
-        prod(0)
-        prod(1)
-        turns(("d", 0, 0), ("d", 0, 1))
+        for n in range(8):
+            prod(n)
+        turns(("d", 0, 0), ("d", 0, 1), ("y", 0, 0, 0), ("y", 0, 0, 1))
         sort_d(1)
-        field(6); field(7)
-        prod(2)
-        prod(3)
-        prod(4)
-        prod(5)
-        field(8)
-        turns(("y", 0, 0, 0), ("y", 0, 0, 1))
-        field(9); field(10)
-        prod(6)
-        prod(7)
-        turns(("d", 1, 0), ("d", 1, 1))
-        field(11)
-        turns(("c", 1, 0), ("c", 1, 1))
+        field(8); field(9); field(10); field(11)
+        turns(("c", 1, 0), ("c", 1, 1), ("d", 1, 0), ("d", 1, 1))
         prod(8)
         prod(9)
-        turns(("d", 2, 0), ("d", 2, 1))
+        turns(("y", 0, 1, 0), ("y", 0, 1, 1))
         sort_d(3)
         quant("fyt", 0, 0)
         prod(10)
         prod(11)
         quant_coef(1, 0)
-        field(16)
-        quant("dt", 0, 0)
         quant_coef(1, 1)
-        field(12); field(13)
-        turns(("y", 0, 1, 0), ("y", 0, 1, 1))
+        field(12); field(13); field(14)
+        turns(("d", 2, 0), ("d", 2, 1))
         quant("fx", 0, 0)
-        field(14); field(15)
-        quant("dt", 1, 0)
-        passes(0, 0, "y0", "x0")
+        quant("dt", 0, 0)
+        field(15)
+        passes(0, 0, "y0", "x0"); passes(1, 0, "y0", "x0")
         prod(12)
+        quant("dt", 1, 0)
         prod(13)
-        turns(("d", 3, 0), ("d", 3, 1))
         quant("fyt", 1, 0)
-        passes(1, 0, "y0", "x0"); passes(2, 0, "y0", "x0")
+        turns(("d", 3, 0), ("d", 3, 1))
+        field(16)
+        passes(0, 0, "y1"); passes(1, 0, "y1")
         prod(14)
         field(17)
-        passes(0, 0, "y1"); passes(1, 0, "y1"); passes(2, 0, "y1")
         prod(15)
-        field(18)
         for t in four:
             late_fy(nc.gpsimd, 1, 0, t)
-        quant("dt", 0, 1)
         quant("fx", 1, 0)
-        passes(0, 0, "x1"); passes(1, 0, "x1"); passes(2, 0, "x1")
+        passes(0, 0, "x1"); passes(1, 0, "x1")
+        passes(2, 0, "y0", "x0", "y1", "x1")
+        field(18)
+        quant("dt", 0, 1)
         quant("dt", 1, 1)
         passes(3, 0, "y0", "x0", "y1", "x1")
         prod(16)
         field(19)
         prod(17)
-        passes(4, 0, "x0", "x1")
+        passes(0, 1, "y0", "y1")
         fin(0, 0)
-        prod(18)
         field(20)
-        passes(5, 0, "x0", "x1")
+        passes(1, 1, "y0", "y1")
+        prod(18)
         fin(1, 0)
+        passes(2, 1, "y0", "y1")
         prod(19)
         field(21)
         fin(2, 0)
-        turns(("y", 1, 1, 0), ("y", 1, 1, 1))
-        passes(6, 0, "x0", "x1")
-        fin(3, 0)
-        field(22)
-        passes(7, 0, "x0", "x1")
-        prod(20)
-        prod(21)
-        turns(("y", 1, 0, 0), ("y", 1, 0, 1))
-        quant("fyt", 1, 1)
-        field(23)
-        passes(4, 0, "y1"); passes(5, 0, "y1"); passes(6, 0, "y1"); passes(7, 0, "y1")
-        prod(22)
-        field(24)
-        passes(0, 1, "y0", "y1")
-        prod(23)
-        quant("fyt", 0, 1)
-        field(25)
-        passes(4, 0, "y0"); passes(5, 0, "y0"); passes(6, 0, "y0"); passes(7, 0, "y0")
-        field(26)
-        prod(24)
-        quant("fx", 0, 1)
-        fin(4, 0)
-        field(27)
-        passes(1, 1, "y0", "y1")
-        fin(5, 0)
-        passes(2, 1, "y0", "y1")
-        prod(25)
         passes(3, 1, "y0", "y1")
-        fin(6, 0)
-        prod(26)
-        passes(0, 1, "x0"); passes(1, 1, "x0"); passes(2, 1, "x0"); passes(3, 1, "x0")
-        prod(27)
-        passes(4, 1, "y0", "y1", "x0")
-        fin(7, 0)
+        field(22)
+        fin(3, 0)
+        prod(20)
         quant("fx", 1, 1)
-        for r in range(5):
-            passes(r, 1, "x1")
-        for r in range(5, 8):
-            passes(r, 1, "y0", "y1", "x0", "x1")
-        for r in range(8):
-            fin(r, 1)
+        turns(("y", 1, 0, 0), ("y", 1, 0, 1))
+        passes(0, 1, "x1"); passes(1, 1, "x1")
+        prod(21)
+        field(23)
+        passes(2, 1, "x1"); passes(3, 1, "x1")
+        prod(22)
+        passes(4, 0, "x0", "x1")
+        late_fy(nc.vector, 1, 1, 0)
+        prod(23)
+        passes(5, 0, "x0", "x1")
+        late_fy(nc.vector, 1, 1, 1)
+        quant("fx", 0, 1)
+        late_fy(nc.vector, 1, 1, 2)
+        late_fy(nc.vector, 1, 1, 3)
+        passes(0, 1, "x0"); passes(1, 1, "x0"); passes(2, 1, "x0"); passes(3, 1, "x0")
+        turns(("y", 1, 1, 0), ("y", 1, 1, 1))
+        quant("fyt", 0, 1)
+        fin(0, 1)
+        passes(4, 0, "y0"); passes(5, 0, "y0")
+        fin(1, 1)
+        fin(2, 1)
+        passes(6, 0, "x0", "x1", "y0")
+        passes(7, 0, "x0", "x1", "y0")
+        quant("fyt", 1, 1)
+        fin(3, 1)
+        for r in range(4, 8):
+            passes(r, 0, "y1")
+        for r in range(4, 8):
+            passes(r, 1, "x0", "x1", "y0", "y1")
+        for h in two:
+            for r in range(4, 8):
+                fin(r, h)

@@ -11,79 +11,93 @@ BF16 = mybir.dt.bfloat16
 I32 = mybir.dt.int32
 U32 = mybir.dt.uint32
 U8 = mybir.dt.uint8
-E4 = mybir.dt.float8_e4m3fn_x4
-E5 = mybir.dt.float8_e5m2_x4
-E2 = mybir.dt.float4_e2m1fn_x4
+E4M3 = mybir.dt.float8_e4m3fn_x4
+E5M2 = mybir.dt.float8_e5m2_x4
+E2M1 = mybir.dt.float4_e2m1fn_x4
 MULT = mybir.AluOpType.mult
 
 P = 128
-H = 512
+HALF = 512
+PAIRS = HALF // 2
+TWO = range(2)
+FOUR = range(4)
+QUADRANTS = [(x, y) for x in TWO for y in TWO]
+UNSORTED_D = 2
+LAST_TILE = (7, 1)
+
+
+def half(x):
+    return slice(HALF * x, HALF * (x + 1))
+
+
+def block(x):
+    return slice(P * x, P * (x + 1))
 
 
 def tile_spectral_flux_divergence_s9_kernel(tc, coef, v_words, v_scales, a, b, d, rjac, out):
     nc = tc.nc
     with ExitStack() as ctx:
-        sb = ctx.enter_context(tc.tile_pool(name="sb", bufs=1))
-        ps = ctx.enter_context(tc.psum_pool(name="ps", bufs=1))
+        sbuf = ctx.enter_context(tc.tile_pool(name="sb", bufs=1))
+        psum = ctx.enter_context(tc.psum_pool(name="ps", bufs=1))
         ctx.enter_context(tc.manual_schedule())
 
-        def sbt(name, shape, dtype):
-            return sb.tile(shape, dtype, name=name, tag=name, align_bytes=64)
+        def sbuf_tile(name, shape, dtype):
+            return sbuf.tile(shape, dtype, name=name, tag=name, align_bytes=64)
 
-        banks = [ps.tile([P, H], F32, name="bank%d" % i, tag="bank%d" % i) for i in range(8)]
-        two = range(2)
-        four = range(4)
-        quads = [(x, y) for x in two for y in two]
+        banks = [psum.tile([P, HALF], F32, name="bank%d" % i, tag="bank%d" % i) for i in range(8)]
 
-        ident = sbt("ident", [P, P], F32)
-        v_plane = sbt("v_plane", [P, N], U8)
-        v_codes = [sbt("v_codes%d" % h, [P, 2 * H], U8) for h in two]
-        coef_raw = {q: sbt("coef_raw%d%d" % q, [P, 2, K], BF16) for q in quads}
-        coef_bf = {q: sbt("coef_bf%d%d" % q, [P, 4 * 256], BF16) for q in quads}
-        coef_q = {q: sbt("coef_q%d%d" % q, [P, 256], U32) for q in quads}
-        coef_s = {q: sbt("coef_s%d%d" % q, [P, 256], U8) for q in quads}
-        d_raw = [sbt("d_raw%d" % rp, [P, 2, N], BF16) for rp in four]
-        kept = {(1, h): sbt("kept1%d" % h, [P, 4, H], F32) for h in two}
-        d_pair = [sbt("d_sorted%d" % rp, [P, 2, N // 2], F32) for rp in two]
-        d_sorted = d_pair + d_pair
-        a_raw = {q: sbt("a_raw%d%d" % q, [P, 4, H], BF16) for q in quads}
-        b_raw = {q: sbt("b_raw%d%d" % q, [P, 4, H], BF16) for q in quads}
-        r_raw = {q: sbt("r_raw%d%d" % q, [P, 4, H], BF16) for q in quads}
-        fy = {(g, h, t): sbt("fy%d%d%d" % (g, h, t), [P, H], BF16) for g, h in quads for t in four}
+        ident = sbuf_tile("ident", [P, P], F32)
+        v_plane = sbuf_tile("v_plane", [P, N], U8)
+        v_codes = [sbuf_tile("v_codes%d" % h, [P, 2 * HALF], U8) for h in TWO]
+
+        coef_raw = {q: sbuf_tile("coef_raw%d%d" % q, [P, 2, K], BF16) for q in QUADRANTS}
+        coef_staged = {q: sbuf_tile("coef_bf%d%d" % q, [P, 4 * 2 * P], BF16) for q in QUADRANTS}
+        coef_codes = {q: sbuf_tile("coef_q%d%d" % q, [P, 2 * P], U32) for q in QUADRANTS}
+        coef_scales = {q: sbuf_tile("coef_s%d%d" % q, [P, 2 * P], U8) for q in QUADRANTS}
+
+        d_raw = [sbuf_tile("d_raw%d" % i, [P, 2, N], BF16) for i in FOUR]
+        d_sorted = [sbuf_tile("d_sorted%d" % i, [P, 2, N // 2], F32) for i in TWO]
+
+        a_raw = {q: sbuf_tile("a_raw%d%d" % q, [P, 4, HALF], BF16) for q in QUADRANTS}
+        b_raw = {q: sbuf_tile("b_raw%d%d" % q, [P, 4, HALF], BF16) for q in QUADRANTS}
+        rjac_raw = {q: sbuf_tile("r_raw%d%d" % q, [P, 4, HALF], BF16) for q in QUADRANTS}
+
+        u_kept = [sbuf_tile("kept1%d" % h, [P, 4, HALF], F32) for h in TWO]
+        fy_rows = {(g, h, t): sbuf_tile("fy%d%d%d" % (g, h, t), [P, HALF], BF16) for g, h in QUADRANTS for t in FOUR}
+
         staged, codes, scales = {}, {}, {}
         for kind in ("dt", "fx", "fyt"):
-            for q in quads:
-                staged[kind, q] = sbt(kind + "_bf%d%d" % q, [P, 4 * H], BF16)
-                codes[kind, q] = sbt(kind + "_q%d%d" % q, [P, H], U32)
-                scales[kind, q] = sbt(kind + "_s%d%d" % q, [P, H], U8)
-        slots = [sbt("res%d" % i, [P, H], F32) for i in range(8)]
-        result = {(r, h): slots[(r % 4) + 4 * h] for r in range(8) for h in two}
+            for q in QUADRANTS:
+                staged[kind, q] = sbuf_tile(kind + "_bf%d%d" % q, [P, 4 * HALF], BF16)
+                codes[kind, q] = sbuf_tile(kind + "_q%d%d" % q, [P, HALF], U32)
+                scales[kind, q] = sbuf_tile(kind + "_s%d%d" % q, [P, HALF], U8)
 
-        def half(x):
-            return slice(H * x, H * (x + 1))
+        results = [sbuf_tile("res%d" % i, [P, HALF], F32) for i in range(8)]
 
-        def load_coef(g, tp):
-            src = coef[half(g), :].rearrange("(p t) k -> p t k", t=4)[:, 2 * tp : 2 * tp + 2, :]
-            nc.sync.dma_start(out=coef_raw[g, tp][:], in_=src)
+        def load_coef(g, j):
+            rows = coef[half(g), :].rearrange("(p t) k -> p t k", t=4)
+            nc.sync.dma_start(out=coef_raw[g, j][:], in_=rows[:, 2 * j : 2 * j + 2, :])
 
         def load_v(h):
-            nc.sync.dma_start(out=v_codes[h][:].bitcast(I32), in_=v_words[0][:, 2 * H * h : 2 * H * (h + 1)].bitcast(I32))
+            words = v_words[0][:, 2 * HALF * h : 2 * HALF * (h + 1)]
+            nc.sync.dma_start(out=v_codes[h][:].bitcast(I32), in_=words.bitcast(I32))
 
         def load_factor(tiles, src, g, h):
             nc.sync.dma_start(out=tiles[g, h][:], in_=src[half(g), half(h)].rearrange("(p t) j -> p t j", t=4))
 
-        def load_d(rp):
-            nc.sync.dma_start(out=d_raw[rp][:], in_=d[256 * rp : 256 * (rp + 1), :].rearrange("(r p) m -> p r m", p=P))
+        def load_d(i):
+            rows = d[2 * P * i : 2 * P * (i + 1), :]
+            nc.sync.dma_start(out=d_raw[i][:], in_=rows.rearrange("(r p) m -> p r m", p=P))
 
         def load_rjac(g, h):
-            nc.sync.dma_start(out=r_raw[g, h][:], in_=rjac[half(g), half(h)].rearrange("(r p) j -> p r j", p=P))
+            nc.sync.dma_start(out=rjac_raw[g, h][:], in_=rjac[half(g), half(h)].rearrange("(r p) j -> p r j", p=P))
 
         nc.vector.memset(v_plane[:].bitcast(U32), 0)
         make_identity(nc, ident[:])
         load_coef(0, 0)
         load_v(0)
         load_coef(0, 1)
-        for q in four:
+        for q in FOUR:
             nc.sync.dma_start(
                 out=v_plane[32 * q : 32 * q + 4, :].bitcast(I32), in_=v_scales[0][4 * q : 4 * q + 4, :].bitcast(I32)
             )
@@ -91,12 +105,12 @@ def tile_spectral_flux_divergence_s9_kernel(tc, coef, v_words, v_scales, a, b, d
         load_d(0)
         load_v(1)
         load_factor(b_raw, b, 0, 1)
-        load_d(1)
-        load_factor(a_raw, a, 0, 0)
         load_coef(1, 0)
         load_coef(1, 1)
-        load_d(2)
+        load_factor(a_raw, a, 0, 0)
+        load_d(1)
         load_factor(a_raw, a, 1, 0)
+        load_d(2)
         load_d(3)
         load_factor(a_raw, a, 1, 1)
         load_factor(b_raw, b, 1, 0)
@@ -107,288 +121,269 @@ def tile_spectral_flux_divergence_s9_kernel(tc, coef, v_words, v_scales, a, b, d
         load_rjac(1, 0)
         load_rjac(1, 1)
 
-        def turn_input(bank, rows, g, dst, engine_copy):
+        def transpose_four(bank, sources):
+            for x, words in enumerate(sources):
+                nc.tensor.transpose(banks[bank][:, block(x)], words, ident[:])
+
+        def interleave_two_row_blocks(bank, dst):
+            nc.scalar.copy(
+                out=dst.bitcast(F32).rearrange("p (r c u) -> p r c u", r=2, u=2),
+                in_=banks[bank][:].rearrange("p (r u c) -> p r c u", r=2, u=2),
+            )
+
+        def every_second_word(rows, s):
             words = rows[:].bitcast(F32)
-            for r in two:
-                for u in two:
-                    x = 2 * r + u
-                    nc.tensor.transpose(bank[:, P * x : P * (x + 1)], words[:, r, 256 * g + u : 256 * (g + 1) : 2], ident[:])
-            engine_copy(
-                out=dst.bitcast(F32).rearrange("p (r c u) -> p r c u", r=2, u=2),
-                in_=bank[:].rearrange("p (r u c) -> p r c u", r=2, u=2),
-            )
+            return [words[:, r, PAIRS * s + u : PAIRS * (s + 1) : 2] for r in TWO for u in TWO]
 
-        def turn_coef(bank, g, tp, engine_copy):
-            turn_input(bank, coef_raw[g, tp], 0, coef_bf[g, tp][:], engine_copy)
+        def turn_coef(g, pair):
+            for j in TWO:
+                transpose_four(pair[j], every_second_word(coef_raw[g, j], 0))
+                interleave_two_row_blocks(pair[j], coef_staged[g, j][:])
 
-        def sort_d(rp):
+        def sort_d(i):
             nc.scalar.copy(
-                out=d_sorted[rp][:].rearrange("p r (g u w) -> p (r g) u w", g=2, u=2),
-                in_=d_raw[rp][:].bitcast(F32).rearrange("p r (g w u) -> p (r g) u w", g=2, u=2),
+                out=d_sorted[i % 2][:].rearrange("p r (s u w) -> p (r s) u w", s=2, u=2),
+                in_=d_raw[i][:].bitcast(F32).rearrange("p r (s w u) -> p (r s) u w", s=2, u=2),
             )
 
-        def turn_d(bank, rp, g):
-            for r in two:
-                for u in two:
-                    x = 2 * r + u
-                    y = 2 * g + u
-                    if rp == 2:
-                        words = d_raw[rp][:].bitcast(F32)[:, r, 256 * g + u : 256 * (g + 1) : 2]
-                    else:
-                        words = d_sorted[rp][:, r, P * y : P * (y + 1)]
-                    nc.tensor.transpose(bank[:, P * x : P * (x + 1)], words, ident[:])
+        def turn_d(i, pair):
+            for s in TWO:
+                if i == UNSORTED_D:
+                    sources = every_second_word(d_raw[i], s)
+                else:
+                    sources = [d_sorted[i % 2][:, r, block(2 * s + u)] for r in TWO for u in TWO]
+                transpose_four(pair[s], sources)
+                width = 4 * 2 * P
+                interleave_two_row_blocks(pair[s], staged["dt", (s, i // 2)][:, width * (i % 2) : width * (i % 2 + 1)])
 
-        def copy_d(bank, rp, g):
-            dst = staged["dt", (g, rp // 2)][:, 1024 * (rp % 2) : 1024 * (rp % 2 + 1)]
-            nc.scalar.copy(
-                out=dst.bitcast(F32).rearrange("p (r c u) -> p r c u", r=2, u=2),
-                in_=bank[:].rearrange("p (r u c) -> p r c u", r=2, u=2),
+        def turn_fy(g, h, pair):
+            for j in TWO:
+                words = [fy_rows[g, h, 2 * j + i][:].bitcast(F32) for i in TWO]
+                transpose_four(pair[j], [words[i][:, block(u)] for i in TWO for u in TWO])
+                dst = staged["fyt", (h, g)][:].bitcast(F32).rearrange("p (c x) -> p c x", x=8)
+                nc.scalar.copy(out=dst[:, :, 4 * j : 4 * j + 4], in_=banks[pair[j]][:].rearrange("p (x c) -> p c x", x=4))
+
+        def quantize_coef(g, j):
+            nc.vector.quantize_mx(
+                out=coef_codes[g, j][:].bitcast(E4M3), scales=coef_scales[g, j][:], in_=coef_staged[g, j][:]
             )
 
-        def td(bank, rp, g):
-            turn_d(bank, rp, g)
-            copy_d(bank, rp, g)
-
-        def keep(n):
-            kind, g, h, x = products[n]
-            nc.scalar.copy(
-                out=kept[g, h][:].rearrange("p t (u c w e) -> p t u c w e", u=2, c=4, e=2)[:, :, :, x, :, :],
-                in_=held[n][:].rearrange("p (t w u e) -> p t u w e", t=4, u=2, e=2),
+        def quantize(kind, s, columns):
+            q = (s, columns)
+            nc.vector.quantize_mx(
+                out=codes[kind, q][:].bitcast(E4M3 if kind == "dt" else E5M2),
+                scales=scales[kind, q][:],
+                in_=staged[kind, q][:],
             )
 
-        def late_fy(engine, g, h, t):
-            engine.tensor_tensor(
-                out=fy[g, h, t][:].rearrange("p (u w e) -> p u w e", u=2, e=2),
-                in0=kept[g, h][:, t, :].rearrange("p (u w e) -> p u w e", u=2, e=2),
-                in1=b_raw[g, h][:, t, :].rearrange("p (w u e) -> p u w e", u=2, e=2),
-                op=MULT,
-            )
-
-        def turn_fy(bank, g, h, tp):
-            for tl in two:
-                words = fy[g, h, 2 * tp + tl][:].bitcast(F32)
-                for u in two:
-                    x = 2 * tl + u
-                    nc.tensor.transpose(bank[:, P * x : P * (x + 1)], words[:, P * u : P * (u + 1)], ident[:])
-            dst = staged["fyt", (h, g)][:].bitcast(F32).rearrange("p (c x) -> p c x", x=8)[:, :, 4 * tp : 4 * tp + 4]
-            nc.scalar.copy(out=dst, in_=bank[:].rearrange("p (x c) -> p c x", x=4))
-
-        def quant_coef(g, tp):
-            nc.vector.quantize_mx(out=coef_q[g, tp][:].bitcast(E4), scales=coef_s[g, tp][:], in_=coef_bf[g, tp][:])
-
-        def quant(kind, x, y):
-            fmt = E4 if kind == "dt" else E5
-            q = (x, y)
-            nc.vector.quantize_mx(out=codes[kind, q][:].bitcast(fmt), scales=scales[kind, q][:], in_=staged[kind, q][:])
-
-        def field_pass(dst, g, t, j0, width):
-            cols = slice(P * (t % 2), P * (t % 2 + 1))
-            h, lo = divmod(j0, H)
+        def field_pass(dst, g, t, first_column, width):
+            columns = block(t % 2)
+            h, lo = divmod(first_column, HALF)
             nc.tensor.matmul_mx(
                 out=dst,
-                lhsT=coef_q[g, t // 2][:, cols].bitcast(E4),
-                lhsT_scale=coef_s[g, t // 2][:, cols],
-                rhs=v_codes[h][:, 2 * lo : 2 * (lo + width)].bitcast(E2),
-                rhs_scale=v_plane[:, j0 : j0 + width],
+                lhsT=coef_codes[g, t // 2][:, columns].bitcast(E4M3),
+                lhsT_scale=coef_scales[g, t // 2][:, columns],
+                rhs=v_codes[h][:, 2 * lo : 2 * (lo + width)].bitcast(E2M1),
+                rhs_scale=v_plane[:, first_column : first_column + width],
                 start=True,
                 stop=True,
             )
 
-        products = (
-            [("fy", 0, h, t) for h in two for t in four]
-            + [("fx", g, h, c) for g, h in ((0, 0), (1, 0), (1, 1), (0, 1)) for c in four]
-        )
+        def field_rows(h, t, bank):
+            field_pass(banks[bank][:], 0, t, HALF * h, HALF)
 
-        idle = list(banks)
-        held = {}
+        def field_columns(g, h, c, bank):
+            for t in FOUR:
+                field_pass(banks[bank][:, block(t)], g, t, HALF * h + P * c, P)
 
-        def field(n):
-            if n >= len(products):
-                return
-            kind, g, h, x = products[n]
-            bank = idle.pop(0)
-            held[n] = bank
-            if kind == "fy":
-                field_pass(bank[:], g, x, H * h, H)
-            else:
-                for t in four:
-                    field_pass(bank[:, P * t : P * (t + 1)], g, t, H * h + P * x, P)
-
-        def product(n):
-            kind, g, h, x = products[n]
-            bank = held[n]
-            if kind == "fy":
-                nc.vector.tensor_tensor(
-                    out=fy[g, h, x][:].rearrange("p (u w e) -> p u w e", u=2, e=2),
-                    in0=bank[:].rearrange("p (w u e) -> p u w e", u=2, e=2),
-                    in1=b_raw[g, h][:, x, :].rearrange("p (w u e) -> p u w e", u=2, e=2),
-                    op=MULT,
-                )
-            else:
-                nc.vector.tensor_tensor(
-                    out=staged["fx", (g, h)][:, H * x : H * (x + 1)].rearrange("p (c i t) -> p c t i", i=2, t=4),
-                    in0=bank[:].rearrange("p (t c i) -> p c t i", t=4, i=2),
-                    in1=a_raw[g, h][:, :, P * x : P * (x + 1)].rearrange("p t (c i) -> p c t i", i=2),
-                    op=MULT,
-                )
-
-        started = set()
-        count = {}
-
-        def flux_pass(bank, r, h, which, s):
-            big, cols = r // 4, slice(P * (r % 4), P * (r % 4 + 1))
-            if which == "x":
-                left, right, lf, rf = ("dt", (s, big)), ("fx", (s, h)), E4, E5
-            else:
-                left, right, lf, rf = ("fyt", (s, big)), ("dt", (s, h)), E5, E4
-            count[r, h] = count.get((r, h), 0) + 1
-            nc.tensor.matmul_mx(
-                out=bank[:],
-                lhsT=codes[left][:, cols].bitcast(lf),
-                lhsT_scale=scales[left][:, cols],
-                rhs=codes[right][:].bitcast(rf),
-                rhs_scale=scales[right][:],
-                start=count[r, h] == 1,
-                stop=count[r, h] == 4,
+        def flux_y(engine, g, h, t, u_sorted):
+            engine.tensor_tensor(
+                out=fy_rows[g, h, t][:].rearrange("p (u w e) -> p u w e", u=2, e=2),
+                in0=u_sorted,
+                in1=b_raw[g, h][:, t, :].rearrange("p (w u e) -> p u w e", u=2, e=2),
+                op=MULT,
             )
 
-        def finish(bank, r, h):
-            pieces = 2 if (r, h) == (7, 1) else 1
-            width = H // pieces
-            for s in range(pieces):
-                cols = slice(width * s, width * (s + 1))
-                nc.vector.tensor_tensor(
-                    out=result[r, h][:, cols], in0=bank[:, cols], in1=r_raw[r // 4, h][:, r % 4, cols], op=MULT
+        def flux_y_from_bank(h, t, bank):
+            flux_y(nc.vector, 0, h, t, banks[bank][:].rearrange("p (w u e) -> p u w e", u=2, e=2))
+
+        def flux_y_from_kept(engine, h, t):
+            flux_y(engine, 1, h, t, u_kept[h][:, t, :].rearrange("p (u w e) -> p u w e", u=2, e=2))
+
+        def flux_x(g, h, c, bank):
+            nc.vector.tensor_tensor(
+                out=staged["fx", (g, h)][:, half(c)].rearrange("p (c i t) -> p c t i", i=2, t=4),
+                in0=banks[bank][:].rearrange("p (t c i) -> p c t i", t=4, i=2),
+                in1=a_raw[g, h][:, :, block(c)].rearrange("p t (c i) -> p c t i", i=2),
+                op=MULT,
+            )
+            if g == 1:
+                nc.scalar.copy(
+                    out=u_kept[h][:].rearrange("p t (u c w e) -> p t u c w e", u=2, c=4, e=2)[:, :, :, c, :, :],
+                    in_=banks[bank][:].rearrange("p (t w u e) -> p t u w e", t=4, u=2, e=2),
                 )
-                nc.sync.dma_start(out=out[P * r : P * (r + 1), half(h)][:, cols], in_=result[r, h][:, cols])
 
-        def step(n):
-            product(n)
+        home, done = {}, {}
 
-        acc = banks[4:8]
-        tb = banks[3]
+        def open_tile(r, h, bank):
+            home[r, h] = banks[bank]
+            done[r, h] = 0
 
-        def passes(r, h, *names):
-            if (r, h) not in held:
-                held[r, h] = idle.pop(0)
-            for w in names:
-                flux_pass(held[r, h], r, h, w[0], int(w[1]))
-
-        def prod(n):
-            product(n)
-            if products[n][0] == "fx" and products[n][1] == 1:
-                keep(n)
-            idle.append(held[n])
-
-        def fin(r, h):
-            finish(held[r, h], r, h)
-            idle.append(held[r, h])
-
-        def turns(*jobs):
-            for job in jobs:
-                bank = idle.pop(0)
-                if job[0] == "c":
-                    turn_coef(bank, job[1], job[2], nc.scalar.copy)
-                elif job[0] == "d":
-                    td(bank, job[1], job[2])
+        def accumulate(r, h, names):
+            g, columns = r // 4, block(r % 4)
+            for name in names.split():
+                s = int(name[1])
+                if name[0] == "x":
+                    left, right, left_format, right_format = ("dt", (s, g)), ("fx", (s, h)), E4M3, E5M2
                 else:
-                    turn_fy(bank, job[1], job[2], job[3])
-                idle.append(bank)
+                    left, right, left_format, right_format = ("fyt", (s, g)), ("dt", (s, h)), E5M2, E4M3
+                done[r, h] = done[r, h] + 1
+                nc.tensor.matmul_mx(
+                    out=home[r, h][:],
+                    lhsT=codes[left][:, columns].bitcast(left_format),
+                    lhsT_scale=scales[left][:, columns],
+                    rhs=codes[right][:].bitcast(right_format),
+                    rhs_scale=scales[right][:],
+                    start=done[r, h] == 1,
+                    stop=done[r, h] == 4,
+                )
 
-        turns(("c", 0, 0), ("c", 0, 1))
-        quant_coef(0, 0)
-        field(0); field(1)
-        quant_coef(0, 1)
-        for n in range(2, 8):
-            field(n)
+        def finish(r, h):
+            result = results[r % 4 + 4 * h]
+            pieces = 2 if (r, h) == LAST_TILE else 1
+            width = HALF // pieces
+            for i in range(pieces):
+                columns = slice(width * i, width * (i + 1))
+                nc.vector.tensor_tensor(
+                    out=result[:, columns], in0=home[r, h][:, columns], in1=rjac_raw[r // 4, h][:, r % 4, columns], op=MULT
+                )
+                nc.sync.dma_start(out=out[block(r), half(h)][:, columns], in_=result[:, columns])
+
+
+        row_bank = {(h, t): (2 + 4 * h + t) % 8 for h in TWO for t in FOUR}
+        turn_coef(0, (0, 1))
+        for j in TWO:
+            quantize_coef(0, j)
+            for t in (2 * j, 2 * j + 1):
+                field_rows(0, t, row_bank[0, t])
+        for t in FOUR:
+            field_rows(1, t, row_bank[1, t])
         sort_d(0)
-        for n in range(8):
-            prod(n)
-        turns(("d", 0, 0), ("d", 0, 1), ("y", 0, 0, 0), ("y", 0, 0, 1))
+        for h in TWO:
+            for t in FOUR:
+                flux_y_from_bank(h, t, row_bank[h, t])
+        turn_d(0, (2, 3))
+        turn_fy(0, 0, (4, 5))
+
+        field_columns(0, 0, 0, 6)
+        field_columns(0, 0, 1, 7)
+        turn_coef(1, (0, 1))
         sort_d(1)
-        field(8); field(9); field(10); field(11)
-        turns(("c", 1, 0), ("c", 1, 1), ("d", 1, 0), ("d", 1, 1))
-        prod(8)
-        prod(9)
-        turns(("y", 0, 1, 0), ("y", 0, 1, 1))
+        field_columns(0, 0, 2, 2)
+        field_columns(0, 0, 3, 3)
+        turn_fy(0, 1, (4, 5))
+        flux_x(0, 0, 0, 6)
+        flux_x(0, 0, 1, 7)
+        quantize_coef(1, 0)
+        quantize("fyt", 0, 0)
+        quantize_coef(1, 1)
+        field_columns(1, 0, 0, 0)
+        field_columns(1, 0, 1, 1)
+        turn_d(1, (6, 7))
         sort_d(3)
-        quant("fyt", 0, 0)
-        prod(10)
-        prod(11)
-        quant_coef(1, 0)
-        quant_coef(1, 1)
-        field(12); field(13); field(14)
-        turns(("d", 2, 0), ("d", 2, 1))
-        quant("fx", 0, 0)
-        quant("dt", 0, 0)
-        field(15)
-        passes(0, 0, "y0", "x0"); passes(1, 0, "y0", "x0")
-        prod(12)
-        quant("dt", 1, 0)
-        prod(13)
-        quant("fyt", 1, 0)
-        turns(("d", 3, 0), ("d", 3, 1))
-        field(16)
-        passes(0, 0, "y1"); passes(1, 0, "y1")
-        prod(14)
-        field(17)
-        prod(15)
-        for t in four:
-            late_fy(nc.gpsimd, 1, 0, t)
-        quant("fx", 1, 0)
-        passes(0, 0, "x1"); passes(1, 0, "x1")
-        passes(2, 0, "y0", "x0", "y1", "x1")
-        field(18)
-        quant("dt", 0, 1)
-        quant("dt", 1, 1)
-        passes(3, 0, "y0", "x0", "y1", "x1")
-        prod(16)
-        field(19)
-        prod(17)
-        passes(0, 1, "y0", "y1")
-        fin(0, 0)
-        field(20)
-        passes(1, 1, "y0", "y1")
-        prod(18)
-        fin(1, 0)
-        passes(2, 1, "y0", "y1")
-        prod(19)
-        field(21)
-        fin(2, 0)
-        passes(3, 1, "y0", "y1")
-        field(22)
-        fin(3, 0)
-        prod(20)
-        quant("fx", 1, 1)
-        turns(("y", 1, 0, 0), ("y", 1, 0, 1))
-        passes(0, 1, "x1"); passes(1, 1, "x1")
-        prod(21)
-        field(23)
-        passes(2, 1, "x1"); passes(3, 1, "x1")
-        prod(22)
-        passes(4, 0, "x0", "x1")
-        late_fy(nc.vector, 1, 1, 0)
-        prod(23)
-        passes(5, 0, "x0", "x1")
-        late_fy(nc.vector, 1, 1, 1)
-        quant("fx", 0, 1)
-        late_fy(nc.vector, 1, 1, 2)
-        late_fy(nc.vector, 1, 1, 3)
-        passes(0, 1, "x0"); passes(1, 1, "x0"); passes(2, 1, "x0"); passes(3, 1, "x0")
-        turns(("y", 1, 1, 0), ("y", 1, 1, 1))
-        quant("fyt", 0, 1)
-        fin(0, 1)
-        passes(4, 0, "y0"); passes(5, 0, "y0")
-        fin(1, 1)
-        fin(2, 1)
-        passes(6, 0, "x0", "x1", "y0")
-        passes(7, 0, "x0", "x1", "y0")
-        quant("fyt", 1, 1)
-        fin(3, 1)
+        flux_x(0, 0, 2, 2)
+        flux_x(0, 0, 3, 3)
+        field_columns(1, 0, 2, 2)
+        field_columns(1, 0, 3, 3)
+        turn_d(2, (4, 5))
+        flux_x(1, 0, 0, 0)
+        quantize("fx", 0, 0)
+        quantize("dt", 0, 0)
+        for r in TWO:
+            open_tile(r, 0, 6 + r)
+            accumulate(r, 0, "y0 x0")
+        flux_x(1, 0, 1, 1)
+        quantize("dt", 1, 0)
+        turn_d(3, (4, 5))
+        flux_x(1, 0, 2, 2)
+        quantize("fyt", 1, 0)
+        for r in TWO:
+            accumulate(r, 0, "y1")
+        open_tile(2, 0, 0)
+        accumulate(2, 0, "y0 x0 y1")
+        flux_x(1, 0, 3, 3)
+
+        for t in FOUR:
+            flux_y_from_kept(nc.gpsimd, 0, t)
+        quantize("fx", 1, 0)
+        for r in range(3):
+            accumulate(r, 0, "x1")
+        field_columns(1, 1, 0, 1)
+        field_columns(1, 1, 1, 4)
+        for s in TWO:
+            quantize("dt", s, 1)
+        open_tile(3, 0, 5)
+        accumulate(3, 0, "y0 x0 y1 x1")
+        finish(0, 0)
+        finish(1, 0)
+        field_columns(1, 1, 2, 2)
+        field_columns(1, 1, 3, 3)
+        open_tile(0, 1, 6)
+        accumulate(0, 1, "y0 y1")
+        flux_x(1, 1, 0, 1)
+        finish(2, 0)
+        open_tile(1, 1, 7)
+        accumulate(1, 1, "y0 y1")
+        flux_x(1, 1, 1, 4)
+        field_columns(0, 1, 0, 1)
+        open_tile(2, 1, 0)
+        accumulate(2, 1, "y0 y1")
+        flux_x(1, 1, 2, 2)
+        finish(3, 0)
+        field_columns(0, 1, 1, 4)
+        open_tile(3, 1, 2)
+        accumulate(3, 1, "y0 y1")
+        flux_x(1, 1, 3, 3)
+        field_columns(0, 1, 2, 5)
+
+        flux_x(0, 1, 0, 1)
+        field_columns(0, 1, 3, 3)
+        quantize("fx", 1, 1)
+        for r in (0, 1):
+            accumulate(r, 1, "x1")
+        flux_x(0, 1, 1, 4)
+        turn_fy(1, 0, (1, 4))
+        for r in (2, 3):
+            accumulate(r, 1, "x1")
+        flux_x(0, 1, 2, 5)
+        flux_x(0, 1, 3, 3)
+        for r, bank in ((4, 5), (5, 3)):
+            open_tile(r, 0, bank)
+            accumulate(r, 0, "x0 x1")
+        flux_y_from_kept(nc.vector, 1, 0)
+        quantize("fx", 0, 1)
+        for t in range(1, 4):
+            flux_y_from_kept(nc.vector, 1, t)
+        for r in FOUR:
+            accumulate(r, 1, "x0")
+        turn_fy(1, 1, (1, 4))
+        quantize("fyt", 0, 1)
+
+        finish(0, 1)
+        for r in (4, 5):
+            accumulate(r, 0, "y0")
+        finish(1, 1)
+        finish(2, 1)
+        for r, bank in ((6, 1), (7, 4)):
+            open_tile(r, 0, bank)
+            accumulate(r, 0, "x0 x1 y0")
+        quantize("fyt", 1, 1)
+        finish(3, 1)
         for r in range(4, 8):
-            passes(r, 0, "y1")
-        for r in range(4, 8):
-            passes(r, 1, "x0", "x1", "y0", "y1")
-        for h in two:
+            accumulate(r, 0, "y1")
+        for r, bank in zip(range(4, 8), (6, 7, 0, 2)):
+            open_tile(r, 1, bank)
+            accumulate(r, 1, "x0 x1 y0 y1")
+        for h in TWO:
             for r in range(4, 8):
-                fin(r, h)
+                finish(r, h)

from contextlib import ExitStack

import concourse.mybir as mybir
from concourse.masks import make_identity

N, K = 1024, 512
FLOPS = 2 * N * K * N + 2 * 2 * N * N * N

F32 = mybir.dt.float32
BF16 = mybir.dt.bfloat16
I32 = mybir.dt.int32
U32 = mybir.dt.uint32
U8 = mybir.dt.uint8
E4M3 = mybir.dt.float8_e4m3fn_x4
E5M2 = mybir.dt.float8_e5m2_x4
E2M1 = mybir.dt.float4_e2m1fn_x4
MULT = mybir.AluOpType.mult

P = 128
HALF = 512
PAIRS = HALF // 2
TWO = range(2)
FOUR = range(4)
QUADRANTS = [(x, y) for x in TWO for y in TWO]
UNSORTED_D = 2
LAST_TILE = (7, 1)


def half(x):
    return slice(HALF * x, HALF * (x + 1))


def block(x):
    return slice(P * x, P * (x + 1))


def tile_spectral_flux_divergence_s9_kernel(tc, coef, v_words, v_scales, a, b, d, rjac, out):
    nc = tc.nc
    with ExitStack() as ctx:
        sbuf = ctx.enter_context(tc.tile_pool(name="sb", bufs=1))
        psum = ctx.enter_context(tc.psum_pool(name="ps", bufs=1))
        ctx.enter_context(tc.manual_schedule())

        def sbuf_tile(name, shape, dtype):
            return sbuf.tile(shape, dtype, name=name, tag=name, align_bytes=64)

        banks = [psum.tile([P, HALF], F32, name="bank%d" % i, tag="bank%d" % i) for i in range(8)]

        ident = sbuf_tile("ident", [P, P], F32)
        v_plane = sbuf_tile("v_plane", [P, N], U8)
        v_codes = [sbuf_tile("v_codes%d" % h, [P, 2 * HALF], U8) for h in TWO]

        coef_raw = {q: sbuf_tile("coef_raw%d%d" % q, [P, 2, K], BF16) for q in QUADRANTS}
        coef_staged = {q: sbuf_tile("coef_bf%d%d" % q, [P, 4 * 2 * P], BF16) for q in QUADRANTS}
        coef_codes = {q: sbuf_tile("coef_q%d%d" % q, [P, 2 * P], U32) for q in QUADRANTS}
        coef_scales = {q: sbuf_tile("coef_s%d%d" % q, [P, 2 * P], U8) for q in QUADRANTS}

        d_raw = [sbuf_tile("d_raw%d" % i, [P, 2, N], BF16) for i in FOUR]
        d_sorted = [sbuf_tile("d_sorted%d" % i, [P, 2, N // 2], F32) for i in TWO]

        a_raw = {q: sbuf_tile("a_raw%d%d" % q, [P, 4, HALF], BF16) for q in QUADRANTS}
        b_raw = {q: sbuf_tile("b_raw%d%d" % q, [P, 4, HALF], BF16) for q in QUADRANTS}
        rjac_raw = {q: sbuf_tile("r_raw%d%d" % q, [P, 4, HALF], BF16) for q in QUADRANTS}

        u_kept = [sbuf_tile("kept1%d" % h, [P, 4, HALF], F32) for h in TWO]
        fy_rows = {(g, h, t): sbuf_tile("fy%d%d%d" % (g, h, t), [P, HALF], BF16) for g, h in QUADRANTS for t in FOUR}

        staged, codes, scales = {}, {}, {}
        for kind in ("dt", "fx", "fyt"):
            for q in QUADRANTS:
                staged[kind, q] = sbuf_tile(kind + "_bf%d%d" % q, [P, 4 * HALF], BF16)
                codes[kind, q] = sbuf_tile(kind + "_q%d%d" % q, [P, HALF], U32)
                scales[kind, q] = sbuf_tile(kind + "_s%d%d" % q, [P, HALF], U8)

        results = [sbuf_tile("res%d" % i, [P, HALF], F32) for i in range(8)]

        def load_coef(g, j):
            rows = coef[half(g), :].rearrange("(p t) k -> p t k", t=4)
            nc.sync.dma_start(out=coef_raw[g, j][:], in_=rows[:, 2 * j : 2 * j + 2, :])

        def load_v(h):
            words = v_words[0][:, 2 * HALF * h : 2 * HALF * (h + 1)]
            nc.sync.dma_start(out=v_codes[h][:].bitcast(I32), in_=words.bitcast(I32))

        def load_factor(tiles, src, g, h):
            nc.sync.dma_start(out=tiles[g, h][:], in_=src[half(g), half(h)].rearrange("(p t) j -> p t j", t=4))

        def load_d(i):
            rows = d[2 * P * i : 2 * P * (i + 1), :]
            nc.sync.dma_start(out=d_raw[i][:], in_=rows.rearrange("(r p) m -> p r m", p=P))

        def load_rjac(g, h):
            nc.sync.dma_start(out=rjac_raw[g, h][:], in_=rjac[half(g), half(h)].rearrange("(r p) j -> p r j", p=P))

        nc.vector.memset(v_plane[:].bitcast(U32), 0)
        make_identity(nc, ident[:])
        load_coef(0, 0)
        load_v(0)
        load_coef(0, 1)
        for q in FOUR:
            nc.sync.dma_start(
                out=v_plane[32 * q : 32 * q + 4, :].bitcast(I32), in_=v_scales[0][4 * q : 4 * q + 4, :].bitcast(I32)
            )
        load_factor(b_raw, b, 0, 0)
        load_d(0)
        load_v(1)
        load_factor(b_raw, b, 0, 1)
        load_coef(1, 0)
        load_coef(1, 1)
        load_factor(a_raw, a, 0, 0)
        load_d(1)
        load_factor(a_raw, a, 1, 0)
        load_d(2)
        load_d(3)
        load_factor(a_raw, a, 1, 1)
        load_factor(b_raw, b, 1, 0)
        load_rjac(0, 0)
        load_factor(a_raw, a, 0, 1)
        load_factor(b_raw, b, 1, 1)
        load_rjac(0, 1)
        load_rjac(1, 0)
        load_rjac(1, 1)

        def transpose_four(bank, sources):
            for x, words in enumerate(sources):
                nc.tensor.transpose(banks[bank][:, block(x)], words, ident[:])

        def interleave_two_row_blocks(bank, dst):
            nc.scalar.copy(
                out=dst.bitcast(F32).rearrange("p (r c u) -> p r c u", r=2, u=2),
                in_=banks[bank][:].rearrange("p (r u c) -> p r c u", r=2, u=2),
            )

        def every_second_word(rows, s):
            words = rows[:].bitcast(F32)
            return [words[:, r, PAIRS * s + u : PAIRS * (s + 1) : 2] for r in TWO for u in TWO]

        def turn_coef(g, pair):
            for j in TWO:
                transpose_four(pair[j], every_second_word(coef_raw[g, j], 0))
                interleave_two_row_blocks(pair[j], coef_staged[g, j][:])

        def sort_d(i):
            nc.scalar.copy(
                out=d_sorted[i % 2][:].rearrange("p r (s u w) -> p (r s) u w", s=2, u=2),
                in_=d_raw[i][:].bitcast(F32).rearrange("p r (s w u) -> p (r s) u w", s=2, u=2),
            )

        def turn_d(i, pair):
            for s in TWO:
                if i == UNSORTED_D:
                    sources = every_second_word(d_raw[i], s)
                else:
                    sources = [d_sorted[i % 2][:, r, block(2 * s + u)] for r in TWO for u in TWO]
                transpose_four(pair[s], sources)
                width = 4 * 2 * P
                interleave_two_row_blocks(pair[s], staged["dt", (s, i // 2)][:, width * (i % 2) : width * (i % 2 + 1)])

        def turn_fy(g, h, pair):
            for j in TWO:
                words = [fy_rows[g, h, 2 * j + i][:].bitcast(F32) for i in TWO]
                transpose_four(pair[j], [words[i][:, block(u)] for i in TWO for u in TWO])
                dst = staged["fyt", (h, g)][:].bitcast(F32).rearrange("p (c x) -> p c x", x=8)
                nc.scalar.copy(out=dst[:, :, 4 * j : 4 * j + 4], in_=banks[pair[j]][:].rearrange("p (x c) -> p c x", x=4))

        def quantize_coef(g, j):
            nc.vector.quantize_mx(
                out=coef_codes[g, j][:].bitcast(E4M3), scales=coef_scales[g, j][:], in_=coef_staged[g, j][:]
            )

        def quantize(kind, s, columns):
            q = (s, columns)
            nc.vector.quantize_mx(
                out=codes[kind, q][:].bitcast(E4M3 if kind == "dt" else E5M2),
                scales=scales[kind, q][:],
                in_=staged[kind, q][:],
            )

        def field_pass(dst, g, t, first_column, width):
            columns = block(t % 2)
            h, lo = divmod(first_column, HALF)
            nc.tensor.matmul_mx(
                out=dst,
                lhsT=coef_codes[g, t // 2][:, columns].bitcast(E4M3),
                lhsT_scale=coef_scales[g, t // 2][:, columns],
                rhs=v_codes[h][:, 2 * lo : 2 * (lo + width)].bitcast(E2M1),
                rhs_scale=v_plane[:, first_column : first_column + width],
                start=True,
                stop=True,
            )

        def field_rows(h, t, bank):
            field_pass(banks[bank][:], 0, t, HALF * h, HALF)

        def field_columns(g, h, c, bank):
            for t in FOUR:
                field_pass(banks[bank][:, block(t)], g, t, HALF * h + P * c, P)

        def flux_y(engine, g, h, t, u_sorted):
            engine.tensor_tensor(
                out=fy_rows[g, h, t][:].rearrange("p (u w e) -> p u w e", u=2, e=2),
                in0=u_sorted,
                in1=b_raw[g, h][:, t, :].rearrange("p (w u e) -> p u w e", u=2, e=2),
                op=MULT,
            )

        def flux_y_from_bank(h, t, bank):
            flux_y(nc.vector, 0, h, t, banks[bank][:].rearrange("p (w u e) -> p u w e", u=2, e=2))

        def flux_y_from_kept(engine, h, t):
            flux_y(engine, 1, h, t, u_kept[h][:, t, :].rearrange("p (u w e) -> p u w e", u=2, e=2))

        def flux_x(g, h, c, bank):
            nc.vector.tensor_tensor(
                out=staged["fx", (g, h)][:, half(c)].rearrange("p (c i t) -> p c t i", i=2, t=4),
                in0=banks[bank][:].rearrange("p (t c i) -> p c t i", t=4, i=2),
                in1=a_raw[g, h][:, :, block(c)].rearrange("p t (c i) -> p c t i", i=2),
                op=MULT,
            )
            if g == 1:
                nc.scalar.copy(
                    out=u_kept[h][:].rearrange("p t (u c w e) -> p t u c w e", u=2, c=4, e=2)[:, :, :, c, :, :],
                    in_=banks[bank][:].rearrange("p (t w u e) -> p t u w e", t=4, u=2, e=2),
                )

        home, done = {}, {}

        def open_tile(r, h, bank):
            home[r, h] = banks[bank]
            done[r, h] = 0

        def accumulate(r, h, names):
            g, columns = r // 4, block(r % 4)
            for name in names.split():
                s = int(name[1])
                if name[0] == "x":
                    left, right, left_format, right_format = ("dt", (s, g)), ("fx", (s, h)), E4M3, E5M2
                else:
                    left, right, left_format, right_format = ("fyt", (s, g)), ("dt", (s, h)), E5M2, E4M3
                done[r, h] = done[r, h] + 1
                nc.tensor.matmul_mx(
                    out=home[r, h][:],
                    lhsT=codes[left][:, columns].bitcast(left_format),
                    lhsT_scale=scales[left][:, columns],
                    rhs=codes[right][:].bitcast(right_format),
                    rhs_scale=scales[right][:],
                    start=done[r, h] == 1,
                    stop=done[r, h] == 4,
                )

        def finish(r, h):
            result = results[r % 4 + 4 * h]
            pieces = 2 if (r, h) == LAST_TILE else 1
            width = HALF // pieces
            for i in range(pieces):
                columns = slice(width * i, width * (i + 1))
                nc.vector.tensor_tensor(
                    out=result[:, columns], in0=home[r, h][:, columns], in1=rjac_raw[r // 4, h][:, r % 4, columns], op=MULT
                )
                nc.sync.dma_start(out=out[block(r), half(h)][:, columns], in_=result[:, columns])


        row_bank = {(h, t): (2 + 4 * h + t) % 8 for h in TWO for t in FOUR}
        turn_coef(0, (0, 1))
        for j in TWO:
            quantize_coef(0, j)
            for t in (2 * j, 2 * j + 1):
                field_rows(0, t, row_bank[0, t])
        for t in FOUR:
            field_rows(1, t, row_bank[1, t])
        sort_d(0)
        for h in TWO:
            for t in FOUR:
                flux_y_from_bank(h, t, row_bank[h, t])
        turn_d(0, (2, 3))
        turn_fy(0, 0, (4, 5))

        field_columns(0, 0, 0, 6)
        field_columns(0, 0, 1, 7)
        turn_coef(1, (0, 1))
        sort_d(1)
        field_columns(0, 0, 2, 2)
        field_columns(0, 0, 3, 3)
        turn_fy(0, 1, (4, 5))
        flux_x(0, 0, 0, 6)
        flux_x(0, 0, 1, 7)
        quantize_coef(1, 0)
        quantize("fyt", 0, 0)
        quantize_coef(1, 1)
        field_columns(1, 0, 0, 0)
        field_columns(1, 0, 1, 1)
        turn_d(1, (6, 7))
        sort_d(3)
        flux_x(0, 0, 2, 2)
        flux_x(0, 0, 3, 3)
        field_columns(1, 0, 2, 2)
        field_columns(1, 0, 3, 3)
        turn_d(2, (4, 5))
        flux_x(1, 0, 0, 0)
        quantize("fx", 0, 0)
        quantize("dt", 0, 0)
        for r in TWO:
            open_tile(r, 0, 6 + r)
            accumulate(r, 0, "y0 x0")
        flux_x(1, 0, 1, 1)
        quantize("dt", 1, 0)
        turn_d(3, (4, 5))
        flux_x(1, 0, 2, 2)
        quantize("fyt", 1, 0)
        for r in TWO:
            accumulate(r, 0, "y1")
        open_tile(2, 0, 0)
        accumulate(2, 0, "y0 x0 y1")
        flux_x(1, 0, 3, 3)

        for t in FOUR:
            flux_y_from_kept(nc.gpsimd, 0, t)
        quantize("fx", 1, 0)
        for r in range(3):
            accumulate(r, 0, "x1")
        field_columns(1, 1, 0, 1)
        field_columns(1, 1, 1, 4)
        for s in TWO:
            quantize("dt", s, 1)
        open_tile(3, 0, 5)
        accumulate(3, 0, "y0 x0 y1 x1")
        finish(0, 0)
        finish(1, 0)
        field_columns(1, 1, 2, 2)
        field_columns(1, 1, 3, 3)
        open_tile(0, 1, 6)
        accumulate(0, 1, "y0 y1")
        flux_x(1, 1, 0, 1)
        finish(2, 0)
        open_tile(1, 1, 7)
        accumulate(1, 1, "y0 y1")
        flux_x(1, 1, 1, 4)
        field_columns(0, 1, 0, 1)
        open_tile(2, 1, 0)
        accumulate(2, 1, "y0 y1")
        flux_x(1, 1, 2, 2)
        finish(3, 0)
        field_columns(0, 1, 1, 4)
        open_tile(3, 1, 2)
        accumulate(3, 1, "y0 y1")
        flux_x(1, 1, 3, 3)
        field_columns(0, 1, 2, 5)

        flux_x(0, 1, 0, 1)
        field_columns(0, 1, 3, 3)
        quantize("fx", 1, 1)
        for r in (0, 1):
            accumulate(r, 1, "x1")
        flux_x(0, 1, 1, 4)
        turn_fy(1, 0, (1, 4))
        for r in (2, 3):
            accumulate(r, 1, "x1")
        flux_x(0, 1, 2, 5)
        flux_x(0, 1, 3, 3)
        for r, bank in ((4, 5), (5, 3)):
            open_tile(r, 0, bank)
            accumulate(r, 0, "x0 x1")
        flux_y_from_kept(nc.vector, 1, 0)
        quantize("fx", 0, 1)
        for t in range(1, 4):
            flux_y_from_kept(nc.vector, 1, t)
        for r in FOUR:
            accumulate(r, 1, "x0")
        turn_fy(1, 1, (1, 4))
        quantize("fyt", 0, 1)

        finish(0, 1)
        for r in (4, 5):
            accumulate(r, 0, "y0")
        finish(1, 1)
        finish(2, 1)
        for r, bank in ((6, 1), (7, 4)):
            open_tile(r, 0, bank)
            accumulate(r, 0, "x0 x1 y0")
        quantize("fyt", 1, 1)
        finish(3, 1)
        for r in range(4, 8):
            accumulate(r, 0, "y1")
        for r, bank in zip(range(4, 8), (6, 7, 0, 2)):
            open_tile(r, 1, bank)
            accumulate(r, 1, "x0 x1 y0 y1")
        for h in TWO:
            for r in range(4, 8):
                finish(r, h)
